import numpy as np, ml_dtypes
CORES = [242,247,114,119]
N = 4
BF = ml_dtypes.bfloat16
S, M, CAP, L = 768, 512, 256, 5
F = 16 // N
def tries(rng, same=False, few=False):
    kid = np.zeros((N, 8, M, 16), np.int32); words = {}; deep = {}
    tid = (rng.integers(1, 65536, (N, 8, M)) * (rng.random((N, 8, M)) < (0.0625 if few else 0.5))).astype(np.int32)
    for q in range(N):
        for g in range(8):
            no = [0, 1] + (2 + rng.permutation(M - 2)).tolist(); pl = rng.random(M).tolist(); cl = rng.integers(0, 16, M).tolist()
            k = kid[q, g]; w = {1: []}; up = []; m = 2; deep[q, g] = []
            for c in (q * F + rng.permutation(F)).tolist()[:1 if few else F]:
                p = 1
                for d in range(L):
                    e = c if d == 0 or same else cl[m]
                    k[no[p], e] = no[m]; w[m] = w[p] + [e]
                    if d < L - 1: up.append(m)
                    p = m; m += 1
                tid[q, g, no[p]] = rng.integers(1, 65536); deep[q, g].append(w[p])
            for m in range(m, M):
                p = up[int(pl[m] * len(up))]; e = cl[m]
                if k[no[p], e]: continue
                k[no[p], e] = no[m]; w[m] = w[p] + [e]
                if len(w[m]) < L: up.append(m)
            words[q, g] = [v for v in w.values() if v]
    tid[:, :, 0] = 0
    return kid.reshape(N, 8, 16 * M), tid, words, deep
def strings(rng, words):
    s = np.zeros((8, N * S), np.int64)
    for g in range(8):
        qs = rng.integers(0, N, N * S).tolist(); ms = rng.random(N * S).tolist(); a = []; i = 0
        while len(a) < N * S:
            v = words[qs[i], g]; a += v[int(ms[i] * len(v))]; i += 1
        s[g] = a[:N * S]
    return np.where(rng.random(s.shape) < 0.1, rng.integers(0, 16, s.shape), s)
def plant(rng, s, deep):
    keep = np.zeros(s.shape, bool)
    for r in range(N):
        for g in range(8):
            v = deep[int(rng.integers(0, N)), g]; j = (r * S + S - 1 - g % (L - 1) + np.arange(L)) % (N * S)
            s[g, j] = v[int(rng.integers(0, len(v)))]; keep[g, j] = True
    return keep
def fit(rng, s, keep, full=False):
    s = s.reshape(8, N, S).transpose(1, 0, 2).astype(np.int32); keep = keep.reshape(8, N, S).transpose(1, 0, 2)
    a, b = int(rng.integers(0, N)), int(rng.integers(0, 8))
    for r in range(N):
        for g in range(8):
            e = s[r, g]; own = e // F; have = np.bincount(own, minlength=N); low = np.bincount(own[keep[r, g]], minlength=N)
            o = rng.permutation(N); i = np.flatnonzero((o == a) if full and g == b else (o != r))[0]; o[[0, i]] = o[[i, 0]]
            want = low.copy() if full else np.minimum(have, CAP)
            if full or (r, g) == (a, b): want[o[0]] = CAP
            for q in np.roll(o, -1): want[q] = min(max(int(want[q]) + S - int(np.sum(want)), int(low[q])), CAP)
            sur = np.concatenate([rng.permutation(np.flatnonzero((own == q) & ~keep[r, g]))[:max(int(have[q] - want[q]), 0)] for q in range(N)])
            need = np.repeat(np.arange(N), np.maximum(want - have, 0))
            e[sur] = need * F + rng.integers(0, F, len(need))
    return np.ascontiguousarray(s)
def setup_inputs(rng):
    kid, tid, words, deep = tries(rng); s = strings(rng, words); keep = plant(rng, s, deep)
    return {"lett": fit(rng, s, keep), "kid": kid, "tid": tid}
def setup_inputs_full(rng):
    kid, tid, words, deep = tries(rng); s = strings(rng, words)
    lett = fit(rng, s, np.zeros(s.shape, bool), True)
    assert np.sum((lett // F)[..., None] == np.arange(N), axis=2).min(axis=0).max() == CAP
    return {"lett": lett, "kid": kid, "tid": tid}
def setup_inputs_runs(rng):
    kid, tid, words, deep = tries(rng, same=True)
    s = np.stack([np.repeat(rng.integers(0, 16, N * S), rng.integers(1, 13, N * S))[:N * S] for g in range(8)]); keep = plant(rng, s, deep)
    return {"lett": fit(rng, s, keep), "kid": kid, "tid": tid}
def setup_inputs_few(rng):
    kid, tid, words, deep = tries(rng, few=True); s = strings(rng, words); keep = plant(rng, s, deep)
    return {"lett": fit(rng, s, keep), "kid": kid, "tid": tid}
def setup_inputs_spread(rng):
    kid = (rng.integers(0, M, (N, 8, M, 16)) * (rng.random((N, 8, M, 16)) > 0.125)).astype(np.int32)
    kid[:, :, 0] = 0; kid[:, :, 1] *= (np.arange(16) // F == np.arange(N)[:, None])[:, None, :]
    tid = (rng.integers(0, 65536, (N, 8, M)) * (rng.random((N, 8, M)) < 0.3)).astype(np.int32); tid[:, :, 0] = 0; tid[:, :, M - 1] = 65535
    s = np.minimum(np.floor(rng.random((8, N * S)) ** 2 * 16), 15).astype(np.int64)
    return {"lett": fit(rng, s, np.zeros(s.shape, bool)), "kid": kid.reshape(N, 8, 16 * M), "tid": tid}
def check_inputs(d):
    bad = []; s, kid, tid = d["lett"], d["kid"], d["tid"]
    if s.min() < 0 or s.max() > 15: bad.append("letters")
    if ((s // F)[..., None] == np.arange(N)).sum(2).max() > CAP: bad.append("slots")
    if kid.min() < 0 or kid.max() >= M: bad.append("children")
    if kid[:, :, :16].any() or tid[:, :, 0].any(): bad.append("node 0")
    if (kid[:, :, 16:32] * (np.arange(16) // F != np.arange(N)[:, None])[:, None, :]).any(): bad.append("roots")
    if tid.min() < 0 or tid.max() > 65535: bad.append("ids")
    return bad
def reference(lett, kid, tid):
    s = np.concatenate(list(lett), axis=1).astype(np.int64)
    own = s // F; g = np.arange(8)[:, None]; node = np.ones(s.shape, np.int64); yl = np.zeros(s.shape, np.int64); yi = np.zeros(s.shape, np.int64)
    for k in range(L):
        node = kid[own, g, 16 * node + np.roll(s, -k, axis=1)].astype(np.int64)
        t = tid[own, g, node]
        yl = np.where(t > 0, k + 1, yl); yi = np.where(t > 0, t, yi)
    yl = np.ascontiguousarray(yl.reshape(8, N, S).transpose(1, 0, 2)); yi = np.ascontiguousarray(yi.reshape(8, N, S).transpose(1, 0, 2))
    return {"ylen": yl.astype(np.float32), "yid": yi.astype(np.float32)}

@@ -1,0 +1,281 @@
+from concourse.bass import DstId, RemoteDMATransfer
+from concourse.mybir import AluOpType as Op, ActivationFunctionType as Act
+
+S, M = 768, 512
+MW = 72
+C = 131072.0
+BIG = 1.5 * 2.0 ** 40
+
+SCRATCH = {
+    "x": ("sbuf", [128, 4, 8, 16], "int32"),
+    "xb": ("sbuf", [128, 8, 4, 16], "bfloat16"),
+    "li": ("sbuf", [128, S], "int32"),
+    "l8": ("sbuf", [128, S], "bfloat16"),
+    "ti": ("sbuf", [128, 32], "int32"),
+    "thi": ("sbuf", [128, 32], "int32"),
+    "tlo": ("sbuf", [128, 32], "int32"),
+    "tz": ("sbuf", [128, 32], "float32"),
+    "rt": ("sbuf", [128, 1], "int32"),
+    "rt2": ("sbuf", [128, 1], "float32"),
+    "sm": ("sbuf", [128, 4 * MW], "bfloat16"),
+    "w": ("sbuf", [128, 4 * M], "bfloat16"),
+    "w2": ("sbuf", [128, 4 * M], "bfloat16"),
+    "e": ("sbuf", [128, S + 16], "bfloat16"),
+    "bm": ("sbuf", [128, S], "bfloat16"),
+    "rm": ("sbuf", [128, S], "bfloat16"),
+    "sel": ("sbuf", [128, 2048], "bfloat16"),
+    "ones": ("sbuf", [128, 16], "bfloat16"),
+    "pi": ("sbuf", [128, 1], "int32"),
+    "gi": ("sbuf", [128, 1], "int32"),
+    "ci": ("sbuf", [128, 1], "int32"),
+    "oi": ("sbuf", [128, 1], "int32"),
+    "rowi": ("sbuf", [128, 128], "int32"),
+    "rowg": ("sbuf", [128, 128], "int32"),
+    "pf": ("sbuf", [128, 1], "float32"),
+    "gf": ("sbuf", [128, 1], "float32"),
+    "cf": ("sbuf", [128, 1], "float32"),
+    "w0": ("sbuf", [128, 1], "float32"),
+    "w1": ("sbuf", [128, 1], "float32"),
+    "wc": ("sbuf", [128, 1], "float32"),
+    "basec": ("sbuf", [128, 1], "float32"),
+    "own": ("sbuf", [128, 1], "float32"),
+    "rootc": ("sbuf", [128, 1], "float32"),
+    "gb": ("sbuf", [128, 128], "bfloat16"),
+    "idb": ("sbuf", [128, 128], "bfloat16"),
+    "idf": ("sbuf", [128, 128], "float32"),
+    "grp": ("sbuf", [128, 8], "float32"),
+    "wg": ("sbuf", [128, 8], "bfloat16"),
+    "baseb": ("sbuf", [128, 48], "bfloat16"),
+    "d5": ("sbuf", [128, 48], "float32"),
+    "rr": ("sbuf", [128, 128], "float32"),
+    "yl": ("sbuf", [128, 128], "float32"),
+    "yi": ("sbuf", [128, 128], "float32"),
+}
+for _k in range(1, 6):
+    SCRATCH["list%d" % _k] = ("sbuf", [128, 48], "uint16")
+    SCRATCH["a%d" % _k] = ("sbuf", [128, S], "bfloat16")
+    SCRATCH["m%d" % _k] = ("sbuf", [128, S], "bfloat16")
+    SCRATCH["t%d" % _k] = ("sbuf", [128, 48], "float32")
+    SCRATCH["d%dm" % _k] = ("sbuf", [128, 48], "float32")
+for _k in range(8):
+    SCRATCH["pb%d" % _k] = ("psum", [128, 512], "float32")
+
+SEMAPHORES = ["ld_lett", "ld_tid", "ld_root", "ld_kid", "sm_arr", "w_arr", "sm_out", "w_out", "w2_in", "st_id", "st_len",
+              "iota", "z_w2", "z_sel", "z_ones", "z_sm", "c_a", "c_b", "c_f", "c_gb", "c_id", "c_grp", "c_w", "c_wc", "c_wg",
+              "c_sel", "s_th", "s_sm", "s_rt", "s_l8", "p_l", "x_conv", "p_x", "w_own", "e_main", "b_mul", "p_base",
+              "b_base", "p_halo", "e_halo", "r_col", "r_mul", "rr_ok", "p_t", "yi_ok", "yl_ok", "d_5"]
+for _k in range(1, 6):
+    SEMAPHORES += ["p_list%d" % _k, "v_list%d" % _k, "v_m%d" % _k, "a_id%d" % _k, "p_z%d" % _k, "v_t%d" % _k, "v_d%d" % _k]
+
+
+def rank_program(g, core, T, topo):
+    rank = T.rank_of(core)
+    if rank is None:
+        return
+    n = len(T.cores)
+    v, pe, act, sp = g.vector, g.tensor, g.scalar, g.sync
+    count = {}
+
+    def inc(call, name, by=1):
+        call.then_inc(T.sem[name], by)
+        count[name] = count.get(name, 0) + by
+
+    def need(queue, *names):
+        for name in names:
+            queue.wait_ge(T.sem[name], count[name])
+
+    near = [d for d in T.cores if d != core and d in topo.cores_of(core)]
+    far = [d for d in T.cores if d != core and d not in topo.cores_of(core)]
+    far_e = [e for e in range(16) if all(e in topo.engines(core, d) for d in far)]
+    near_e = [e for e in range(16) if all(e in topo.engines(core, d) for d in near) and e not in far_e]
+
+    def spread(ap, arr, out):
+        tr = []
+        for ds, es in ((far, far_e), (near, near_e)):
+            ids = []
+            for d in ds:
+                rid, pid = topo.addr(d, core)
+                ids.append(DstId(rid=rid, pnc=pid))
+            tr.append(RemoteDMATransfer(dst_ids=ids, dma_engine_mask=sum(1 << e for e in es), remote_sem=T.sem[arr],
+                                        srcs=[ap], dsts=[ap for _ in ds]))
+            count[out] = count.get(out, 0) + len(es)
+            count[arr] = count.get(arr, 0) + len(es) * len(ds)
+        g.remote_dma_fused(tr, local_sem=T.sem[out])
+
+    c0 = MW * rank
+    cw = M * rank
+    inc(sp.dma_start(T.ti[:, :], T.tid[:, :]), "ld_tid", 16)
+    inc(act.dma_start(T.rt[:, :], T.kid[:, 16:32]), "ld_root", 16)
+    inc(sp.dma_start(T.li[0:8, :], T.lett[:, :]), "ld_lett", 16)
+    for q4 in range(4):
+        for a, queue in ((0, sp), (1, act)):
+            h = 4 * a + q4
+            inc(queue.dma_start(T.x[64 * a:64 * a + 64, q4, :, :], T.kid[h:h + 1, :]), "ld_kid", 16)
+
+    inc(g.iota(T.pi[:, :], [[0, 1]], 0, 1), "iota")
+    inc(g.iota(T.rowi[:, :], [[1, 128]], 0, 0), "iota")
+    inc(v.memset(T.sm[:, c0 + 64:c0 + MW], 0.0), "z_sm")
+    inc(v.memset(T.ones[:, :], 1.0), "z_ones")
+    inc(v.memset(T.sel[:, :], 0.0), "z_sel")
+    need(v, "iota")
+    inc(v.tensor_scalar(T.gi[:, :], T.pi[:, :], 4, None, Op.arith_shift_right), "c_a")
+    inc(v.tensor_scalar(T.ci[:, :], T.pi[:, :], 15, None, Op.bitwise_and), "c_a")
+    inc(v.tensor_scalar(T.rowg[:, :], T.rowi[:, :], 4, None, Op.arith_shift_right), "c_a")
+    inc(v.tensor_copy(T.pf[:, :], T.pi[:, :]), "c_a")
+    need(v, "c_a")
+    inc(v.tensor_scalar(T.oi[:, :], T.ci[:, :], 2, None, Op.arith_shift_right), "c_b")
+    inc(v.tensor_copy(T.gf[:, :], T.gi[:, :]), "c_b")
+    inc(v.tensor_copy(T.cf[:, :], T.ci[:, :]), "c_b")
+    inc(v.tensor_scalar(T.gb[0:8, :], T.rowg[0:8, :], T.pf[0:8, :], None, Op.is_equal), "c_gb")
+    inc(v.tensor_scalar(T.idb[:, :], T.rowi[:, :], T.pf[:, :], None, Op.is_equal), "c_id")
+    inc(v.tensor_scalar(T.idf[:, :], T.rowi[:, :], T.pf[:, :], None, Op.is_equal), "c_id")
+    need(v, "c_b")
+    inc(v.tensor_scalar(T.own[:, :], T.oi[:, :], float(rank), None, Op.is_equal), "c_f")
+    inc(v.tensor_scalar(T.basec[:, :], T.oi[:, :], 512.0, 256.0, Op.mult, Op.add), "c_f")
+    inc(v.tensor_scalar(T.grp[:, :], T.rowi[:, 0:8], T.gf[:, :], None, Op.is_equal), "c_grp")
+    inc(v.tensor_scalar(T.w0[:, :], T.cf[:, :], 0.0, 256.0, Op.is_equal, Op.mult), "c_w")
+    inc(v.tensor_scalar(T.w1[:, :], T.cf[:, :], 1.0, None, Op.is_equal), "c_w")
+    need(v, "c_grp", "c_w", "z_sel", "z_ones")
+    inc(v.tensor_tensor(T.wc[:, :], T.w0[:, :], T.w1[:, :], Op.add), "c_wc")
+    for h in range(8):
+        inc(v.tensor_scalar(T.sel[:, 16 * h:2048:129], T.ones[:, :], T.grp[:, h:h + 1], None, Op.mult), "c_sel")
+    need(v, "c_wc")
+    inc(v.tensor_scalar(T.wg[:, :], T.grp[:, :], T.wc[:, :], None, Op.mult), "c_wg")
+
+    need(v, "ld_tid")
+    inc(v.tensor_scalar(T.thi[:, :], T.ti[:, :], 8, None, Op.arith_shift_right), "s_th")
+    inc(v.tensor_scalar(T.tlo[:, :], T.ti[:, :], 255, None, Op.bitwise_and), "s_th")
+    inc(v.tensor_scalar(T.tz[:, :], T.ti[:, :], 0.0, -65536.0, Op.is_equal, Op.mult), "s_th")
+    need(v, "ld_root", "c_f", "z_sm")
+    inc(v.tensor_scalar(T.sm[:, c0 + 64:c0 + 65], T.rt[:, :], -256.0, T.own[:, :], Op.add, Op.mult), "s_sm")
+    need(v, "s_th")
+    inc(v.tensor_tensor(T.sm[:, c0:c0 + 32], T.thi[:, :], T.tz[:, :], Op.add), "s_sm")
+    inc(v.tensor_copy(T.sm[:, c0 + 32:c0 + 64], T.tlo[:, :]), "s_sm")
+    need(v, "ld_lett")
+    inc(v.tensor_copy(T.sm[0:8, c0 + 68:c0 + 72], T.li[0:8, 0:4]), "s_sm")
+    need(g, "s_sm")
+    spread(T.sm[:, c0:c0 + MW], "sm_arr", "sm_out")
+    inc(v.tensor_copy(T.l8[0:8, :], T.li[0:8, :]), "s_l8")
+    need(pe, "s_l8", "c_gb")
+    for j in range(2):
+        inc(pe.matmul(T["pb%d" % j][:, 0:384], T.gb[0:8, :], T.l8[0:8, 384 * j:384 * j + 384], True, True), "p_l")
+
+    need(v, "ld_kid")
+    for q4 in range(4):
+        inc(v.tensor_scalar(T.xb[:, :, q4, :], T.x[:, q4, :, :], -256.0, None, Op.add), "x_conv")
+    need(pe, "x_conv", "c_id")
+    for ml in range(8):
+        for a in range(2):
+            p = slice(64 * a, 64 * a + 64)
+            inc(pe.matmul(T.pb2[p, ml:512:8], T.xb[p, ml, :, :], T.idb[p, p], True, True), "p_x")
+    need(v, "p_x")
+    inc(v.tensor_copy(T.w[:, cw:cw + M], T.pb2[:, :]), "w_own")
+    need(g, "w_own")
+    spread(T.w[:, cw:cw + M], "w_arr", "w_out")
+
+    inc(v.memset(T.w2[:, :], 0.0), "z_w2")
+    need(v, "p_l")
+    for j in range(2):
+        inc(v.tensor_scalar(T.e[:, 384 * j:384 * j + 384], T["pb%d" % j][:, 0:384], T.cf[:, :], None, Op.is_equal), "e_main")
+    need(v, "e_main")
+    inc(v.tensor_scalar(T.bm[:, :], T.e[:, 0:S], T.basec[:, :], None, Op.mult), "b_mul")
+
+    def wrap(src, col, done, based):
+        o = T.pb4[:, col:col + 48] if based else T.pb6[:, 0:48]
+        if based:
+            pe.matmul(o, T.idb[:, :], T.baseb[:, :], True, False)
+        for i in range(16):
+            call = pe.matmul(o, T.sel[:, 128 * i:128 * i + 128], src[:, i:S:16], i == 0 and not based, i == 15)
+        inc(call, done)
+
+    need(pe, "c_sel", "b_mul")
+    wrap(T.bm, 0, "p_base", False)
+    need(v, "p_base")
+    inc(v.tensor_copy(T.baseb[:, :], T.pb6[:, 0:48]), "b_base")
+
+    need(sp, "z_w2", "s_sm")
+    need(act, "z_w2", "s_sm")
+    for j in range(n):
+        q = (rank + j) % n
+        if j == 1:
+            need(sp, "sm_arr")
+            need(act, "sm_arr")
+        inc(sp.dma_start(T.w2[0:128:16, M * q:M * q + M], T.sm[:, MW * q:MW * q + 32]), "w2_in", 16)
+        inc(act.dma_start(T.w2[1:128:16, M * q:M * q + M], T.sm[:, MW * q + 32:MW * q + 64]), "w2_in", 16)
+    cn = MW * ((rank + 1) % n)
+    need(pe, "sm_arr")
+    inc(pe.matmul(T.pb5[:, 0:4], T.gb[0:8, :], T.sm[0:8, cn + 68:cn + 72], True, True), "p_halo")
+    need(v, "sm_arr")
+    from_all = T.sm[:, 64:4 * MW:MW]
+    inc(v.tensor_reduce(T.rootc[:, :], from_all, AX, Op.add), "r_col")
+    need(v, "r_col")
+    inc(v.tensor_scalar(T.rm[:, :], T.e[:, 0:S], T.rootc[:, :], None, Op.mult), "r_mul")
+    need(v, "p_halo")
+    inc(v.tensor_scalar(T.e[:, S:S + 4], T.pb5[:, 0:4], T.cf[:, :], None, Op.is_equal), "e_halo")
+    need(pe, "r_mul", "b_base")
+    wrap(T.rm, 0, "p_list1", True)
+
+    win, win2 = T.w[:, 0:4 * M], T.w2[:, 0:4 * M]
+    need(v, "e_halo", "w_own")
+    zb = {1: T.pb5, 2: T.pb6, 3: T.pb7, 4: T.pb0, 5: T.pb1}
+
+    def keep(k):
+        need(v, "p_z%d" % k)
+        if k == 1:
+            inc(v.tensor_scalar(T.d1m[:, :], zb[1][:, 0:48], -C, -C, Op.max, Op.add), "v_d1")
+            return
+        need(v, "v_d%d" % (k - 1))
+        if k == 5:
+            inc(v.tensor_tensor(T.d5[:, :], zb[5][:, 0:48], T.d4m[:, :], Op.max), "d_5")
+            return
+        inc(v.tensor_tensor(T["t%d" % k][:, :], zb[k][:, 0:48], T["d%dm" % (k - 1)][:, :], Op.max), "v_t%d" % k)
+        need(v, "v_t%d" % k)
+        inc(v.tensor_scalar(T["d%dm" % k][:, :], T["t%d" % k][:, :], -C, None, Op.add), "v_d%d" % k)
+
+    for k in range(1, 6):
+        lst, a = T["list%d" % k], T["a%d" % k]
+        need(v, "p_list%d" % k)
+        inc(v.tensor_copy(lst[:, :], T.pb4[:, 48 * (k - 1):48 * k]), "v_list%d" % k)
+        need(v, "v_list%d" % k)
+        need(act, "v_list%d" % k)
+        if k == 1:
+            need(act, "w2_in")
+            need(v, "w_arr")
+        if k < 5:
+            mk = T["m%d" % k]
+            inc(v.tensor_tensor(mk[:, :], win.indirect(lst[:, 0:48]), T.e[:, k:k + S], Op.mult), "v_m%d" % k)
+            inc(act.activation(a[:, :], win2.indirect(lst[:, 0:48]), Act.Copy), "a_id%d" % k)
+            need(pe, "v_m%d" % k)
+            wrap(mk, 48 * k, "p_list%d" % (k + 1), True)
+        else:
+            need(v, "w2_in")
+            inc(v.tensor_copy(a[:, 0:384], win2.indirect(lst[:, 0:24])), "a_id5")
+            inc(act.activation(a[:, 384:768], win2.indirect(lst[:, 24:48]), Act.Copy), "a_id5")
+        need(pe, "a_id%d" % k)
+        if k == 1:
+            need(pe, "c_wg")
+        for b in range(6):
+            inc(pe.matmul(zb[k][:, b:48:6], a[:, 128 * b:128 * b + 128], T.wg[:, :], True, True), "p_z%d" % k)
+        if k > 1:
+            keep(k - 1)
+    keep(5)
+
+    need(pe, "d_5")
+    inc(pe.transpose(T.pb3[0:48, 0:128], T.d5[:, :], T.idf[:, :]), "p_t")
+    need(v, "p_t")
+    inc(v.tensor_scalar(T.rr[0:48, :], T.pb3[0:48, 0:128], BIG, -BIG, Op.add, Op.add), "rr_ok")
+    need(v, "rr_ok")
+    inc(v.tensor_tensor(T.yi[0:48, :], T.pb3[0:48, 0:128], T.rr[0:48, :], Op.subtract), "yi_ok")
+    need(act, "rr_ok")
+    inc(act.activation(T.yl[0:48, :], T.rr[0:48, :], Act.Copy, bias=5.0, scale=1.0 / C), "yl_ok")
+    need(act, "yl_ok")
+    inc(act.dma_start(T.ylen[:, :], T.yl[0:48, :]), "st_len", 16)
+    need(sp, "yi_ok")
+    inc(sp.dma_start(T.yid[:, :], T.yi[0:48, :]), "st_id", 16)
+    need(act, "st_len")
+    need(sp, "st_id")
+    need(g, "sm_out", "w_out")
+
+
+from concourse.mybir import AxisListType
+AX = AxisListType.X

@@ -1,56 +1,18 @@
 from concourse.bass import DstId, RemoteDMATransfer
-from concourse.mybir import AluOpType as Op, ActivationFunctionType as Act
+from concourse.mybir import AluOpType as Op, ActivationFunctionType as Act, AxisListType
 
 S, M = 768, 512
-MW = 72
+MW = 24
 C = 131072.0
 BIG = 1.5 * 2.0 ** 40
-
-SCRATCH = {
-    "x": ("sbuf", [128, 4, 8, 16], "int32"),
-    "xb": ("sbuf", [128, 8, 4, 16], "bfloat16"),
-    "li": ("sbuf", [128, S], "int32"),
-    "l8": ("sbuf", [128, S], "bfloat16"),
-    "ti": ("sbuf", [128, 32], "int32"),
-    "thi": ("sbuf", [128, 32], "int32"),
-    "tlo": ("sbuf", [128, 32], "int32"),
-    "tz": ("sbuf", [128, 32], "float32"),
-    "rt": ("sbuf", [128, 1], "int32"),
-    "rt2": ("sbuf", [128, 1], "float32"),
-    "sm": ("sbuf", [128, 4 * MW], "bfloat16"),
-    "w": ("sbuf", [128, 4 * M], "bfloat16"),
-    "w2": ("sbuf", [128, 4 * M], "bfloat16"),
-    "e": ("sbuf", [128, S + 16], "bfloat16"),
-    "bm": ("sbuf", [128, S], "bfloat16"),
-    "rm": ("sbuf", [128, S], "bfloat16"),
-    "sel": ("sbuf", [128, 2048], "bfloat16"),
-    "ones": ("sbuf", [128, 16], "bfloat16"),
-    "pi": ("sbuf", [128, 1], "int32"),
-    "gi": ("sbuf", [128, 1], "int32"),
-    "ci": ("sbuf", [128, 1], "int32"),
-    "oi": ("sbuf", [128, 1], "int32"),
-    "rowi": ("sbuf", [128, 128], "int32"),
-    "rowg": ("sbuf", [128, 128], "int32"),
-    "pf": ("sbuf", [128, 1], "float32"),
-    "gf": ("sbuf", [128, 1], "float32"),
-    "cf": ("sbuf", [128, 1], "float32"),
-    "w0": ("sbuf", [128, 1], "float32"),
-    "w1": ("sbuf", [128, 1], "float32"),
-    "wc": ("sbuf", [128, 1], "float32"),
-    "basec": ("sbuf", [128, 1], "float32"),
-    "own": ("sbuf", [128, 1], "float32"),
-    "rootc": ("sbuf", [128, 1], "float32"),
-    "gb": ("sbuf", [128, 128], "bfloat16"),
-    "idb": ("sbuf", [128, 128], "bfloat16"),
-    "idf": ("sbuf", [128, 128], "float32"),
-    "grp": ("sbuf", [128, 8], "float32"),
-    "wg": ("sbuf", [128, 8], "bfloat16"),
-    "baseb": ("sbuf", [128, 48], "bfloat16"),
-    "d5": ("sbuf", [128, 48], "float32"),
-    "rr": ("sbuf", [128, 128], "float32"),
-    "yl": ("sbuf", [128, 128], "float32"),
-    "yi": ("sbuf", [128, 128], "float32"),
-}
+SCRATCH = {"x": ("sbuf", [128, 4, 8, 16], "int32"), "xb": ("sbuf", [128, 8, 4, 16], "bfloat16"),
+           "idh": ("dram", [4, 128, 32], "bfloat16"), "idl": ("dram", [4, 128, 32], "bfloat16")}
+for _t, _s in (("int32", "li768 ti32 thi32 tlo32 rt16 pi1 gi1 ci1 oi1 rowi128 rowg128"),
+               ("float32", "tz32 rd16 diag16 pf1 gf1 cf1 ncf1 wz1 wy1 wc1 basec1 rootc1 idf128 grp8 d48 rr128 yl128 yi128"),
+               ("bfloat16", "l768 hi32 lo32 sm96 w2048 v2048 ab768 e784 bm768 rm768 sel2048 ones16 gb128 idb128 wg8 baseb48")):
+    for _n in _s.split():
+        _b = _n.rstrip("0123456789")
+        SCRATCH[_b] = ("sbuf", [128, int(_n[len(_b):])], _t)
 for _k in range(1, 6):
     SCRATCH["list%d" % _k] = ("sbuf", [128, 48], "uint16")
     SCRATCH["a%d" % _k] = ("sbuf", [128, S], "bfloat16")
@@ -59,13 +21,11 @@ for _k in range(1, 6):
     SCRATCH["d%dm" % _k] = ("sbuf", [128, 48], "float32")
 for _k in range(8):
     SCRATCH["pb%d" % _k] = ("psum", [128, 512], "float32")
-
-SEMAPHORES = ["ld_lett", "ld_tid", "ld_root", "ld_kid", "sm_arr", "w_arr", "sm_out", "w_out", "w2_in", "st_id", "st_len",
-              "iota", "z_w2", "z_sel", "z_ones", "z_sm", "c_a", "c_b", "c_f", "c_gb", "c_id", "c_grp", "c_w", "c_wc", "c_wg",
-              "c_sel", "s_th", "s_sm", "s_rt", "s_l8", "p_l", "x_conv", "p_x", "w_own", "e_main", "b_mul", "p_base",
-              "b_base", "p_halo", "e_halo", "r_col", "r_mul", "rr_ok", "p_t", "yi_ok", "yl_ok", "d_5"]
+SEMAPHORES = ("ld_lett ld_tid ld_root ld_kid sm_arr w_arr id_arr sm_out w_out id_out w2_in st_id st_len iota z_w2 z_sel z_ones "
+              "z_sm c_a c_b c_f c_dg c_gb c_id c_idf c_grp c_w c_wc c_wg c_sel s_th s_id s_sm s_l8 p_l0 p_l1 x_conv0 x_conv1 p_x0 "
+              "p_x1 w_own e_abs e_main b_mul p_base b_base p_halo e_halo r_diag r_col r_mul rr_ok p_t yi_ok yl_ok d_5 a_id6").split()
 for _k in range(1, 6):
-    SEMAPHORES += ["p_list%d" % _k, "v_list%d" % _k, "v_m%d" % _k, "a_id%d" % _k, "p_z%d" % _k, "v_t%d" % _k, "v_d%d" % _k]
+    SEMAPHORES += [_n % _k for _n in ("p_list%d", "v_list%d", "v_m%d", "a_id%d", "p_z%d", "v_t%d", "v_d%d")]
 
 
 def rank_program(g, core, T, topo):
@@ -84,153 +44,177 @@ def rank_program(g, core, T, topo):
         for name in names:
             queue.wait_ge(T.sem[name], count[name])
 
+    def ts(name, out, in0, s1, op0, s2=None, op1=None):
+        inc(v.tensor_scalar(out, in0, s1, None, op0) if op1 is None else v.tensor_scalar(out, in0, s1, s2, op0, op1), name)
+
     near = [d for d in T.cores if d != core and d in topo.cores_of(core)]
     far = [d for d in T.cores if d != core and d not in topo.cores_of(core)]
     far_e = [e for e in range(16) if all(e in topo.engines(core, d) for d in far)]
     near_e = [e for e in range(16) if all(e in topo.engines(core, d) for d in near) and e not in far_e]
+    near_e = near_e[:len(far_e) * len(near) // len(far)]
 
-    def spread(ap, arr, out):
-        tr = []
+    def spread(pieces, arr, out):
+        tr, k = [], len(pieces)
         for ds, es in ((far, far_e), (near, near_e)):
             ids = []
             for d in ds:
                 rid, pid = topo.addr(d, core)
                 ids.append(DstId(rid=rid, pnc=pid))
-            tr.append(RemoteDMATransfer(dst_ids=ids, dma_engine_mask=sum(1 << e for e in es), remote_sem=T.sem[arr],
-                                        srcs=[ap], dsts=[ap for _ in ds]))
+            w = len(es) // k
+            for j, (src, dst) in enumerate(pieces):
+                tr.append(RemoteDMATransfer(dst_ids=ids, dma_engine_mask=sum(1 << e for e in es[w * j:w * j + w]),
+                                            remote_sem=T.sem[arr], srcs=[src], dsts=[dst for _ in ds]))
             count[out] = count.get(out, 0) + len(es)
             count[arr] = count.get(arr, 0) + len(es) * len(ds)
         g.remote_dma_fused(tr, local_sem=T.sem[out])
 
-    c0 = MW * rank
-    cw = M * rank
-    inc(sp.dma_start(T.ti[:, :], T.tid[:, :]), "ld_tid", 16)
-    inc(act.dma_start(T.rt[:, :], T.kid[:, 16:32]), "ld_root", 16)
+    c0, cw, o = MW * rank, M * rank, 4 * rank
     inc(sp.dma_start(T.li[0:8, :], T.lett[:, :]), "ld_lett", 16)
+    inc(act.dma_start(T.rt[0:8, :], T.kid[:, 16:32]), "ld_root", 16)
     for q4 in range(4):
         for a, queue in ((0, sp), (1, act)):
             h = 4 * a + q4
             inc(queue.dma_start(T.x[64 * a:64 * a + 64, q4, :, :], T.kid[h:h + 1, :]), "ld_kid", 16)
+    inc(sp.dma_start(T.ti[:, :], T.tid[:, :]), "ld_tid", 16)
 
     inc(g.iota(T.pi[:, :], [[0, 1]], 0, 1), "iota")
     inc(g.iota(T.rowi[:, :], [[1, 128]], 0, 0), "iota")
-    inc(v.memset(T.sm[:, c0 + 64:c0 + MW], 0.0), "z_sm")
-    inc(v.memset(T.ones[:, :], 1.0), "z_ones")
     inc(v.memset(T.sel[:, :], 0.0), "z_sel")
+    inc(v.memset(T.sm[:, c0:c0 + MW], 0.0), "z_sm")
+    inc(v.memset(T.ones[:, :], 1.0), "z_ones")
+    need(act, "z_sel")
+    inc(act.activation(T.v[:, :], T.sel[:, :], Act.Copy), "z_w2")
     need(v, "iota")
-    inc(v.tensor_scalar(T.gi[:, :], T.pi[:, :], 4, None, Op.arith_shift_right), "c_a")
-    inc(v.tensor_scalar(T.ci[:, :], T.pi[:, :], 15, None, Op.bitwise_and), "c_a")
-    inc(v.tensor_scalar(T.rowg[:, :], T.rowi[:, :], 4, None, Op.arith_shift_right), "c_a")
+    ts("c_a", T.gi[:, :], T.pi[:, :], 4, Op.arith_shift_right)
+    ts("c_a", T.ci[:, :], T.pi[:, :], 15, Op.bitwise_and)
+    ts("c_a", T.rowg[:, :], T.rowi[:, :], 4, Op.arith_shift_right)
     inc(v.tensor_copy(T.pf[:, :], T.pi[:, :]), "c_a")
     need(v, "c_a")
-    inc(v.tensor_scalar(T.oi[:, :], T.ci[:, :], 2, None, Op.arith_shift_right), "c_b")
     inc(v.tensor_copy(T.gf[:, :], T.gi[:, :]), "c_b")
     inc(v.tensor_copy(T.cf[:, :], T.ci[:, :]), "c_b")
-    inc(v.tensor_scalar(T.gb[0:8, :], T.rowg[0:8, :], T.pf[0:8, :], None, Op.is_equal), "c_gb")
-    inc(v.tensor_scalar(T.idb[:, :], T.rowi[:, :], T.pf[:, :], None, Op.is_equal), "c_id")
-    inc(v.tensor_scalar(T.idf[:, :], T.rowi[:, :], T.pf[:, :], None, Op.is_equal), "c_id")
-    need(v, "c_b")
-    inc(v.tensor_scalar(T.own[:, :], T.oi[:, :], float(rank), None, Op.is_equal), "c_f")
-    inc(v.tensor_scalar(T.basec[:, :], T.oi[:, :], 512.0, 256.0, Op.mult, Op.add), "c_f")
-    inc(v.tensor_scalar(T.grp[:, :], T.rowi[:, 0:8], T.gf[:, :], None, Op.is_equal), "c_grp")
-    inc(v.tensor_scalar(T.w0[:, :], T.cf[:, :], 0.0, 256.0, Op.is_equal, Op.mult), "c_w")
-    inc(v.tensor_scalar(T.w1[:, :], T.cf[:, :], 1.0, None, Op.is_equal), "c_w")
-    need(v, "c_grp", "c_w", "z_sel", "z_ones")
-    inc(v.tensor_tensor(T.wc[:, :], T.w0[:, :], T.w1[:, :], Op.add), "c_wc")
-    for h in range(8):
-        inc(v.tensor_scalar(T.sel[:, 16 * h:2048:129], T.ones[:, :], T.grp[:, h:h + 1], None, Op.mult), "c_sel")
-    need(v, "c_wc")
-    inc(v.tensor_scalar(T.wg[:, :], T.grp[:, :], T.wc[:, :], None, Op.mult), "c_wg")
+    ts("c_b", T.ncf[:, :], T.ci[:, :], -1.0, Op.mult)
+    ts("c_b", T.oi[:, :], T.ci[:, :], 2, Op.arith_shift_right)
+    ts("c_gb", T.gb[0:8, :], T.rowg[0:8, :], T.pf[0:8, :], Op.is_equal)
+    ts("c_id", T.idb[:, :], T.rowi[:, :], T.pf[:, :], Op.is_equal)
 
-    need(v, "ld_tid")
-    inc(v.tensor_scalar(T.thi[:, :], T.ti[:, :], 8, None, Op.arith_shift_right), "s_th")
-    inc(v.tensor_scalar(T.tlo[:, :], T.ti[:, :], 255, None, Op.bitwise_and), "s_th")
-    inc(v.tensor_scalar(T.tz[:, :], T.ti[:, :], 0.0, -65536.0, Op.is_equal, Op.mult), "s_th")
-    need(v, "ld_root", "c_f", "z_sm")
-    inc(v.tensor_scalar(T.sm[:, c0 + 64:c0 + 65], T.rt[:, :], -256.0, T.own[:, :], Op.add, Op.mult), "s_sm")
-    need(v, "s_th")
-    inc(v.tensor_tensor(T.sm[:, c0:c0 + 32], T.thi[:, :], T.tz[:, :], Op.add), "s_sm")
-    inc(v.tensor_copy(T.sm[:, c0 + 32:c0 + 64], T.tlo[:, :]), "s_sm")
+    need(v, "ld_root", "z_sm")
+    ts("s_sm", T.sm[0:8, c0 + o:c0 + o + 4], T.rt[0:8, o:o + 4], -256.0, Op.add)
     need(v, "ld_lett")
-    inc(v.tensor_copy(T.sm[0:8, c0 + 68:c0 + 72], T.li[0:8, 0:4]), "s_sm")
+    inc(v.tensor_copy(T.sm[0:8, c0 + 16:c0 + 20], T.li[0:8, 0:4]), "s_sm")
     need(g, "s_sm")
-    spread(T.sm[:, c0:c0 + MW], "sm_arr", "sm_out")
-    inc(v.tensor_copy(T.l8[0:8, :], T.li[0:8, :]), "s_l8")
+    spread([(T.sm[:, c0:c0 + MW], T.sm[:, c0:c0 + MW])], "sm_arr", "sm_out")
+    inc(v.tensor_copy(T.l[0:8, :], T.li[0:8, :]), "s_l8")
     need(pe, "s_l8", "c_gb")
     for j in range(2):
-        inc(pe.matmul(T["pb%d" % j][:, 0:384], T.gb[0:8, :], T.l8[0:8, 384 * j:384 * j + 384], True, True), "p_l")
+        inc(pe.matmul(T["pb%d" % j][:, 0:384], T.gb[0:8, :], T.l[0:8, 384 * j:384 * j + 384], True, True), "p_l%d" % j)
+    need(v, "c_b")
+    ts("c_f", T.basec[:, :], T.oi[:, :], 512.0, Op.mult, 256.0, Op.add)
+
+    need(act, "c_b")
+    for j in range(2):
+        need(act, "p_l%d" % j)
+        inc(act.activation(T.ab[:, 384 * j:384 * j + 384], T["pb%d" % j][:, 0:384], Act.Abs, bias=T.ncf[:, :]), "e_abs")
+    need(act, "e_abs")
+    inc(act.activation(T.e[:, 0:S], T.ab[:, :], Act.Relu, bias=1.0, scale=-1.0), "e_main")
+    need(act, "e_main", "c_f")
+    inc(act.activation(T.bm[:, :], T.e[:, 0:S], Act.Copy, scale=T.basec[:, :]), "b_mul")
 
     need(v, "ld_kid")
-    for q4 in range(4):
-        inc(v.tensor_scalar(T.xb[:, :, q4, :], T.x[:, q4, :, :], -256.0, None, Op.add), "x_conv")
-    need(pe, "x_conv", "c_id")
-    for ml in range(8):
-        for a in range(2):
-            p = slice(64 * a, 64 * a + 64)
-            inc(pe.matmul(T.pb2[p, ml:512:8], T.xb[p, ml, :, :], T.idb[p, p], True, True), "p_x")
-    need(v, "p_x")
-    inc(v.tensor_copy(T.w[:, cw:cw + M], T.pb2[:, :]), "w_own")
+    for par in range(2):
+        for q4 in range(4):
+            ts("x_conv%d" % par, T.xb[:, par:8:2, q4, :], T.x[:, q4, par:8:2, :], -256.0, Op.add)
+    need(pe, "c_id")
+    for par in range(2):
+        need(pe, "x_conv%d" % par)
+        for ml in range(par, 8, 2):
+            for a in range(2):
+                p = slice(64 * a, 64 * a + 64)
+                inc(pe.matmul(T["pb%d" % (2 + par)][p, ml // 2:256:4], T.xb[p, ml, :, :], T.idb[p, p], True, True), "p_x%d" % par)
+        need(v, "p_x%d" % par)
+        inc(v.tensor_copy(T.w[:, cw + par:cw + M:2], T["pb%d" % (2 + par)][:, 0:256]), "w_own")
     need(g, "w_own")
-    spread(T.w[:, cw:cw + M], "w_arr", "w_out")
+    spread([(T.w[:, cw:cw + M], T.w[:, cw:cw + M])], "w_arr", "w_out")
 
-    inc(v.memset(T.w2[:, :], 0.0), "z_w2")
-    need(v, "p_l")
-    for j in range(2):
-        inc(v.tensor_scalar(T.e[:, 384 * j:384 * j + 384], T["pb%d" % j][:, 0:384], T.cf[:, :], None, Op.is_equal), "e_main")
-    need(v, "e_main")
-    inc(v.tensor_scalar(T.bm[:, :], T.e[:, 0:S], T.basec[:, :], None, Op.mult), "b_mul")
+    ts("c_grp", T.grp[:, :], T.rowi[:, 0:8], T.gf[:, :], Op.is_equal)
+    need(v, "c_grp", "z_sel", "z_ones", "z_w2")
+    for h in range(8):
+        ts("c_sel", T.sel[:, 16 * h:2048:129], T.ones[:, :], T.grp[:, h:h + 1], Op.mult)
+    ts("c_dg", T.diag[:, :], T.rowi[:, 0:16], T.cf[:, :], Op.is_equal)
 
-    def wrap(src, col, done, based):
+    need(v, "ld_tid")
+    ts("s_th", T.thi[:, :], T.ti[:, :], 8, Op.arith_shift_right)
+    ts("s_th", T.tlo[:, :], T.ti[:, :], 255, Op.bitwise_and)
+    ts("s_th", T.tz[:, :], T.ti[:, :], 0.0, Op.is_equal, -65536.0, Op.mult)
+    need(v, "s_th")
+    inc(v.tensor_tensor(T.hi[:, :], T.thi[:, :], T.tz[:, :], Op.add), "s_id")
+    inc(v.tensor_copy(T.lo[:, :], T.tlo[:, :]), "s_id")
+    need(g, "s_id")
+    spread([(T.hi[:, :], T.idh[rank]), (T.lo[:, :], T.idl[rank])], "id_arr", "id_out")
+
+    def wrap(src, col, done, based, after):
         o = T.pb4[:, col:col + 48] if based else T.pb6[:, 0:48]
         if based:
             pe.matmul(o, T.idb[:, :], T.baseb[:, :], True, False)
+        need(pe, after)
         for i in range(16):
             call = pe.matmul(o, T.sel[:, 128 * i:128 * i + 128], src[:, i:S:16], i == 0 and not based, i == 15)
         inc(call, done)
 
-    need(pe, "c_sel", "b_mul")
-    wrap(T.bm, 0, "p_base", False)
-    need(v, "p_base")
-    inc(v.tensor_copy(T.baseb[:, :], T.pb6[:, 0:48]), "b_base")
+    need(pe, "c_sel")
+    wrap(T.bm, 0, "p_base", False, "b_mul")
+    need(act, "p_base")
+    inc(act.activation(T.baseb[:, :], T.pb6[:, 0:48], Act.Copy), "b_base")
 
-    need(sp, "z_w2", "s_sm")
-    need(act, "z_w2", "s_sm")
-    for j in range(n):
-        q = (rank + j) % n
-        if j == 1:
-            need(sp, "sm_arr")
-            need(act, "sm_arr")
-        inc(sp.dma_start(T.w2[0:128:16, M * q:M * q + M], T.sm[:, MW * q:MW * q + 32]), "w2_in", 16)
-        inc(act.dma_start(T.w2[1:128:16, M * q:M * q + M], T.sm[:, MW * q + 32:MW * q + 64]), "w2_in", 16)
     cn = MW * ((rank + 1) % n)
     need(pe, "sm_arr")
-    inc(pe.matmul(T.pb5[:, 0:4], T.gb[0:8, :], T.sm[0:8, cn + 68:cn + 72], True, True), "p_halo")
-    need(v, "sm_arr")
-    from_all = T.sm[:, 64:4 * MW:MW]
-    inc(v.tensor_reduce(T.rootc[:, :], from_all, AX, Op.add), "r_col")
-    need(v, "r_col")
-    inc(v.tensor_scalar(T.rm[:, :], T.e[:, 0:S], T.rootc[:, :], None, Op.mult), "r_mul")
-    need(v, "p_halo")
-    inc(v.tensor_scalar(T.e[:, S:S + 4], T.pb5[:, 0:4], T.cf[:, :], None, Op.is_equal), "e_halo")
-    need(pe, "r_mul", "b_base")
-    wrap(T.rm, 0, "p_list1", True)
+    inc(pe.matmul(T.pb5[:, 0:4], T.gb[0:8, :], T.sm[0:8, cn + 16:cn + 20], True, True), "p_halo")
+    for q in range(n):
+        call = pe.matmul(T.pb5[:, 8:24], T.gb[0:8, :], T.sm[0:8, MW * q:MW * q + 16], q == 0, q == n - 1)
+    inc(call, "p_halo")
+    need(v, "p_halo", "c_dg")
+    inc(v.tensor_tensor(T.rd[:, :], T.pb5[:, 8:24], T.diag[:, :], Op.mult), "r_diag")
+    need(v, "r_diag")
+    inc(v.tensor_reduce(T.rootc[:, :], T.rd[:, :], AxisListType.X, Op.add), "r_col")
+    need(v, "r_col", "e_main")
+    ts("r_mul", T.rm[:, :], T.e[:, 0:S], T.rootc[:, :], Op.mult)
+    ts("e_halo", T.e[:, S:S + 4], T.pb5[:, 0:4], T.cf[:, :], Op.is_equal)
 
-    win, win2 = T.w[:, 0:4 * M], T.w2[:, 0:4 * M]
+    for queue, row, own, land in ((sp, 0, T.hi, T.idh), (act, 1, T.lo, T.idl)):
+        need(queue, "z_w2", "s_id", "id_arr")
+        inc(queue.dma_start(T.v[row:128:16, cw:cw + M], own[:, :]), "w2_in", 16)
+        for j in range(1, n):
+            q = (rank + j) % n
+            inc(queue.dma_start(T.v[row:128:16, M * q:M * q + M], land[q]), "w2_in", 16)
+    need(pe, "b_base")
+    wrap(T.rm, 0, "p_list1", True, "r_mul")
+
+    win, win2 = T.w[:, 0:4 * M], T.v[:, 0:4 * M]
     need(v, "e_halo", "w_own")
     zb = {1: T.pb5, 2: T.pb6, 3: T.pb7, 4: T.pb0, 5: T.pb1}
 
     def keep(k):
         need(v, "p_z%d" % k)
         if k == 1:
-            inc(v.tensor_scalar(T.d1m[:, :], zb[1][:, 0:48], -C, -C, Op.max, Op.add), "v_d1")
+            ts("v_d1", T.d1m[:, :], zb[1][:, 0:48], -C, Op.max, -C, Op.add)
             return
         need(v, "v_d%d" % (k - 1))
         if k == 5:
-            inc(v.tensor_tensor(T.d5[:, :], zb[5][:, 0:48], T.d4m[:, :], Op.max), "d_5")
+            inc(v.tensor_tensor(T.d[:, :], zb[5][:, 0:48], T.d4m[:, :], Op.max), "d_5")
             return
         inc(v.tensor_tensor(T["t%d" % k][:, :], zb[k][:, 0:48], T["d%dm" % (k - 1)][:, :], Op.max), "v_t%d" % k)
         need(v, "v_t%d" % k)
-        inc(v.tensor_scalar(T["d%dm" % k][:, :], T["t%d" % k][:, :], -C, None, Op.add), "v_d%d" % k)
+        ts("v_d%d" % k, T["d%dm" % k][:, :], T["t%d" % k][:, :], -C, Op.add)
+
+    def ids(*ks):
+        for k in ks:
+            a = T["a%d" % k]
+            need(pe, "a_id%d" % k)
+            if k == 1:
+                need(pe, "c_wg")
+            for b in range(6):
+                if k == 5 and b == 3:
+                    need(pe, "a_id6")
+                inc(pe.matmul(zb[k][:, b:48:6], a[:, 128 * b:128 * b + 128], T.wg[:, :], True, True), "p_z%d" % k)
 
     for k in range(1, 6):
         lst, a = T["list%d" % k], T["a%d" % k]
@@ -245,25 +229,35 @@ def rank_program(g, core, T, topo):
             mk = T["m%d" % k]
             inc(v.tensor_tensor(mk[:, :], win.indirect(lst[:, 0:48]), T.e[:, k:k + S], Op.mult), "v_m%d" % k)
             inc(act.activation(a[:, :], win2.indirect(lst[:, 0:48]), Act.Copy), "a_id%d" % k)
-            need(pe, "v_m%d" % k)
-            wrap(mk, 48 * k, "p_list%d" % (k + 1), True)
+            need(pe, "v_list%d" % k)
+            wrap(mk, 48 * k, "p_list%d" % (k + 1), True, "v_m%d" % k)
+            if k == 1:
+                ts("c_w", T.wz[:, :], T.cf[:, :], 0.0, Op.is_equal, 256.0, Op.mult)
+                ts("c_w", T.wy[:, :], T.cf[:, :], 1.0, Op.is_equal)
+                ts("c_idf", T.idf[:, :], T.rowi[:, :], T.pf[:, :], Op.is_equal)
+                need(v, "c_w")
+                inc(v.tensor_tensor(T.wc[:, :], T.wz[:, :], T.wy[:, :], Op.add), "c_wc")
+                need(v, "c_wc")
+                ts("c_wg", T.wg[:, :], T.grp[:, :], T.wc[:, :], Op.mult)
+            if k == 3:
+                ids(1, 2)
+            if k == 4:
+                keep(1)
+                keep(2)
+                ids(3, 4)
         else:
             need(v, "w2_in")
             inc(v.tensor_copy(a[:, 0:384], win2.indirect(lst[:, 0:24])), "a_id5")
-            inc(act.activation(a[:, 384:768], win2.indirect(lst[:, 24:48]), Act.Copy), "a_id5")
-        need(pe, "a_id%d" % k)
-        if k == 1:
-            need(pe, "c_wg")
-        for b in range(6):
-            inc(pe.matmul(zb[k][:, b:48:6], a[:, 128 * b:128 * b + 128], T.wg[:, :], True, True), "p_z%d" % k)
-        if k > 1:
-            keep(k - 1)
+            inc(act.activation(a[:, 384:768], win2.indirect(lst[:, 24:48]), Act.Copy), "a_id6")
+            ids(5)
+            keep(3)
+            keep(4)
     keep(5)
 
-    need(pe, "d_5")
-    inc(pe.transpose(T.pb3[0:48, 0:128], T.d5[:, :], T.idf[:, :]), "p_t")
+    need(pe, "d_5", "c_idf")
+    inc(pe.transpose(T.pb3[0:48, 0:128], T.d[:, :], T.idf[:, :]), "p_t")
     need(v, "p_t")
-    inc(v.tensor_scalar(T.rr[0:48, :], T.pb3[0:48, 0:128], BIG, -BIG, Op.add, Op.add), "rr_ok")
+    ts("rr_ok", T.rr[0:48, :], T.pb3[0:48, 0:128], BIG, Op.add, -BIG, Op.add)
     need(v, "rr_ok")
     inc(v.tensor_tensor(T.yi[0:48, :], T.pb3[0:48, 0:128], T.rr[0:48, :], Op.subtract), "yi_ok")
     need(act, "rr_ok")
@@ -274,8 +268,4 @@ def rank_program(g, core, T, topo):
     inc(sp.dma_start(T.yid[:, :], T.yi[0:48, :]), "st_id", 16)
     need(act, "st_len")
     need(sp, "st_id")
-    need(g, "sm_out", "w_out")
-
-
-from concourse.mybir import AxisListType
-AX = AxisListType.X
+    need(g, "sm_out", "w_out", "id_out")

@@ -2,14 +2,17 @@ from concourse.bass import DstId, RemoteDMATransfer
 from concourse.mybir import AluOpType as Op, ActivationFunctionType as Act, AxisListType
 
 S, M = 768, 512
-MW = 24
+MW = 32
 C = 131072.0
 BIG = 1.5 * 2.0 ** 40
 SCRATCH = {"x": ("sbuf", [128, 4, 8, 16], "int32"), "xb": ("sbuf", [128, 8, 4, 16], "bfloat16"),
            "idh": ("dram", [4, 128, 32], "bfloat16"), "idl": ("dram", [4, 128, 32], "bfloat16")}
-for _t, _s in (("int32", "li768 ti32 thi32 tlo32 rt16 pi1 gi1 ci1 oi1 rowi128 rowg128"),
-               ("float32", "tz32 rd16 diag16 pf1 gf1 cf1 ncf1 wz1 wy1 wc1 basec1 rootc1 idf128 grp8 d48 rr128 yl128 yi128"),
-               ("bfloat16", "l768 hi32 lo32 sm96 w2048 v2048 ab768 e784 bm768 rm768 sel2048 ones16 gb128 idb128 wg8 baseb48")):
+for _t, _s in (("int32", "li768 ti32 thi32 tlo32 rt16 pi1 gi1 ci1 oi1 rowi128 rowg128 ln48 lq48 lk48 lc48"),
+               ("float32", "tz32 rd16 diag16 dgown16 rx16 pf1 gf1 cf1 cown1 ncf1 wz1 wy1 wc1 basec1 lcol1 oix1 rootc1 roott1 "
+                           "idf128 grp8 d48 rr128 yl128 yi128"),
+               ("uint16", "rown2 rall2 letl48 letc48"),
+               ("bfloat16", "l768 hi32 lo32 sm128 w2048 v2048 ab768 e784 bm768 sel2048 ones16 gb128 idb128 wg8 baseb48 "
+                            "rtmp16 r32 rid16")):
     for _n in _s.split():
         _b = _n.rstrip("0123456789")
         SCRATCH[_b] = ("sbuf", [128, int(_n[len(_b):])], _t)
@@ -21,9 +24,10 @@ for _k in range(1, 6):
     SCRATCH["d%dm" % _k] = ("sbuf", [128, 48], "float32")
 for _k in range(8):
     SCRATCH["pb%d" % _k] = ("psum", [128, 512], "float32")
-SEMAPHORES = ("ld_lett ld_tid ld_root ld_kid sm_arr w_arr id_arr sm_out w_out id_out w2_in st_id st_len iota z_w2 z_sel z_ones "
-              "z_sm c_a c_b c_f c_dg c_gb c_id c_idf c_grp c_w c_wc c_wg c_sel s_th s_id s_sm s_l8 p_l0 p_l1 x_conv0 x_conv1 p_x0 "
-              "p_x1 w_own e_abs e_main b_mul p_base b_base p_halo e_halo r_diag r_col r_mul rr_ok p_t yi_ok yl_ok d_5 a_id6").split()
+SEMAPHORES = ("ld_lett ld_tid ld_root ld_kid sm_arr w_arr r_arr sm_out w_out r_out w2_in st_id st_len iota z_w2 z_sel z_ones "
+              "z_sm c_a c_b c_f c_lc c_dg c_do c_gb c_id c_idf c_grp c_w c_wc c_wg c_sel s_th s_sm s_l0 s_l1 p_l0 p_l1 p_own o_rx "
+              "o_rt o_ls x_conv0 x_conv1 p_x0 p_x1 w_own r_tmp r_own e_abs e_main b_mul p_base l_n l_l l_q l_k l_c l_cc b_base "
+              "p_halo e_halo r_diag r_col r_all a_rid rr_ok p_t yi_ok yl_ok d_5 a_id6").split()
 for _k in range(1, 6):
     SEMAPHORES += [_n % _k for _n in ("p_list%d", "v_list%d", "v_m%d", "a_id%d", "p_z%d", "v_t%d", "v_d%d")]
 
@@ -54,28 +58,30 @@ def rank_program(g, core, T, topo):
     near_e = near_e[:len(far_e) * len(near) // len(far)]
 
     def spread(pieces, arr, out):
-        tr, k = [], len(pieces)
+        tr = []
         for ds, es in ((far, far_e), (near, near_e)):
             ids = []
             for d in ds:
                 rid, pid = topo.addr(d, core)
                 ids.append(DstId(rid=rid, pnc=pid))
-            w = len(es) // k
-            for j, (src, dst) in enumerate(pieces):
-                tr.append(RemoteDMATransfer(dst_ids=ids, dma_engine_mask=sum(1 << e for e in es[w * j:w * j + w]),
+            at = 0
+            for src, dst, share in pieces:
+                w = len(es) // share
+                tr.append(RemoteDMATransfer(dst_ids=ids, dma_engine_mask=sum(1 << e for e in es[at:at + w]),
                                             remote_sem=T.sem[arr], srcs=[src], dsts=[dst for _ in ds]))
-            count[out] = count.get(out, 0) + len(es)
-            count[arr] = count.get(arr, 0) + len(es) * len(ds)
+                at += w
+            count[out] = count.get(out, 0) + at
+            count[arr] = count.get(arr, 0) + at * len(ds)
         g.remote_dma_fused(tr, local_sem=T.sem[out])
 
     c0, cw, o = MW * rank, M * rank, 4 * rank
-    inc(sp.dma_start(T.li[0:8, :], T.lett[:, :]), "ld_lett", 16)
     inc(act.dma_start(T.rt[0:8, :], T.kid[:, 16:32]), "ld_root", 16)
+    inc(sp.dma_start(T.li[0:8, :], T.lett[:, :]), "ld_lett", 16)
+    inc(sp.dma_start(T.ti[:, :], T.tid[:, :]), "ld_tid", 16)
     for q4 in range(4):
         for a, queue in ((0, sp), (1, act)):
             h = 4 * a + q4
             inc(queue.dma_start(T.x[64 * a:64 * a + 64, q4, :, :], T.kid[h:h + 1, :]), "ld_kid", 16)
-    inc(sp.dma_start(T.ti[:, :], T.tid[:, :]), "ld_tid", 16)
 
     inc(g.iota(T.pi[:, :], [[0, 1]], 0, 1), "iota")
     inc(g.iota(T.rowi[:, :], [[1, 128]], 0, 0), "iota")
@@ -93,6 +99,7 @@ def rank_program(g, core, T, topo):
     inc(v.tensor_copy(T.gf[:, :], T.gi[:, :]), "c_b")
     inc(v.tensor_copy(T.cf[:, :], T.ci[:, :]), "c_b")
     ts("c_b", T.ncf[:, :], T.ci[:, :], -1.0, Op.mult)
+    ts("c_b", T.cown[:, :], T.ci[:, :], float(o), Op.add)
     ts("c_b", T.oi[:, :], T.ci[:, :], 2, Op.arith_shift_right)
     ts("c_gb", T.gb[0:8, :], T.rowg[0:8, :], T.pf[0:8, :], Op.is_equal)
     ts("c_id", T.idb[:, :], T.rowi[:, :], T.pf[:, :], Op.is_equal)
@@ -101,14 +108,34 @@ def rank_program(g, core, T, topo):
     ts("s_sm", T.sm[0:8, c0 + o:c0 + o + 4], T.rt[0:8, o:o + 4], -256.0, Op.add)
     need(v, "ld_lett")
     inc(v.tensor_copy(T.sm[0:8, c0 + 16:c0 + 20], T.li[0:8, 0:4]), "s_sm")
+    need(v, "ld_tid")
+    ts("s_th", T.thi[:, :], T.ti[:, :], 8, Op.arith_shift_right)
+    ts("s_th", T.tlo[:, :], T.ti[:, :], 255, Op.bitwise_and)
+    ts("s_th", T.tz[:, :], T.ti[:, :], 0.0, Op.is_equal, -65536.0, Op.mult)
+    need(v, "s_th")
+    inc(v.tensor_tensor(T.hi[:, :], T.thi[:, :], T.tz[:, :], Op.add), "s_sm")
+    inc(v.tensor_copy(T.lo[:, :], T.tlo[:, :]), "s_sm")
     need(g, "s_sm")
-    spread([(T.sm[:, c0:c0 + MW], T.sm[:, c0:c0 + MW])], "sm_arr", "sm_out")
-    inc(v.tensor_copy(T.l[0:8, :], T.li[0:8, :]), "s_l8")
-    need(pe, "s_l8", "c_gb")
+    spread([(T.sm[:, c0:c0 + MW], T.sm[:, c0:c0 + MW], 2), (T.hi[:, :], T.idh[rank], 4), (T.lo[:, :], T.idl[rank], 4)],
+           "sm_arr", "sm_out")
+    need(pe, "s_sm", "c_gb")
+    inc(pe.matmul(T.pb7[:, 0:16], T.gb[0:8, :], T.sm[0:8, c0:c0 + 16], True, True), "p_own")
     for j in range(2):
+        inc(v.tensor_copy(T.l[0:8, 384 * j:384 * j + 384], T.li[0:8, 384 * j:384 * j + 384]), "s_l%d" % j)
+        need(pe, "s_l%d" % j)
         inc(pe.matmul(T["pb%d" % j][:, 0:384], T.gb[0:8, :], T.l[0:8, 384 * j:384 * j + 384], True, True), "p_l%d" % j)
     need(v, "c_b")
+    ts("c_do", T.dgown[:, :], T.rowi[:, 0:16], T.cown[:, :], Op.is_equal)
     ts("c_f", T.basec[:, :], T.oi[:, :], 512.0, Op.mult, 256.0, Op.add)
+    ts("c_f", T.oix[:, :], T.oi[:, :], 4.0, Op.mult)
+    need(v, "c_do", "c_f", "p_own")
+    inc(v.tensor_tensor(T.rx[:, :], T.pb7[:, 0:16], T.dgown[:, :], Op.mult), "o_rx")
+    inc(v.tensor_tensor(T.lcol[:, :], T.oix[:, :], T.cf[:, :], Op.add), "c_lc")
+    ts("c_grp", T.grp[:, :], T.rowi[:, 0:8], T.gf[:, :], Op.is_equal)
+    need(v, "o_rx")
+    inc(v.tensor_reduce(T.roott[:, :], T.rx[:, :], AxisListType.X, Op.add), "o_rt")
+    need(v, "o_rt")
+    ts("o_ls", T.rown[:, 0:1], T.roott[:, :], 256.0, Op.add)
 
     need(act, "c_b")
     for j in range(2):
@@ -116,40 +143,34 @@ def rank_program(g, core, T, topo):
         inc(act.activation(T.ab[:, 384 * j:384 * j + 384], T["pb%d" % j][:, 0:384], Act.Abs, bias=T.ncf[:, :]), "e_abs")
     need(act, "e_abs")
     inc(act.activation(T.e[:, 0:S], T.ab[:, :], Act.Relu, bias=1.0, scale=-1.0), "e_main")
-    need(act, "e_main", "c_f")
-    inc(act.activation(T.bm[:, :], T.e[:, 0:S], Act.Copy, scale=T.basec[:, :]), "b_mul")
+    need(act, "e_main", "c_lc")
+    inc(act.activation(T.bm[:, :], T.e[:, 0:S], Act.Copy, scale=T.lcol[:, :]), "b_mul")
 
     need(v, "ld_kid")
     for par in range(2):
         for q4 in range(4):
             ts("x_conv%d" % par, T.xb[:, par:8:2, q4, :], T.x[:, q4, par:8:2, :], -256.0, Op.add)
     need(pe, "c_id")
+    need(v, "c_grp", "z_sel", "z_ones", "z_w2")
     for par in range(2):
         need(pe, "x_conv%d" % par)
         for ml in range(par, 8, 2):
             for a in range(2):
                 p = slice(64 * a, 64 * a + 64)
                 inc(pe.matmul(T["pb%d" % (2 + par)][p, ml // 2:256:4], T.xb[p, ml, :, :], T.idb[p, p], True, True), "p_x%d" % par)
+        for h in range(4 * par, 4 * par + 4):
+            ts("c_sel", T.sel[:, 16 * h:2048:129], T.ones[:, :], T.grp[:, h:h + 1], Op.mult)
         need(v, "p_x%d" % par)
         inc(v.tensor_copy(T.w[:, cw + par:cw + M:2], T["pb%d" % (2 + par)][:, 0:256]), "w_own")
+    need(v, "w_own", "o_ls")
+    inc(v.tensor_copy(T.rtmp[:, :], T.w[:, cw:cw + M].indirect(T.rown[:, 0:1])), "r_tmp")
+    need(g, "r_tmp")
+    spread([(T.rtmp[:, 0:8], T.r[:, 8 * rank:8 * rank + 8], 1)], "r_arr", "r_out")
     need(g, "w_own")
-    spread([(T.w[:, cw:cw + M], T.w[:, cw:cw + M])], "w_arr", "w_out")
-
-    ts("c_grp", T.grp[:, :], T.rowi[:, 0:8], T.gf[:, :], Op.is_equal)
-    need(v, "c_grp", "z_sel", "z_ones", "z_w2")
-    for h in range(8):
-        ts("c_sel", T.sel[:, 16 * h:2048:129], T.ones[:, :], T.grp[:, h:h + 1], Op.mult)
+    spread([(T.w[:, cw:cw + M], T.w[:, cw:cw + M], 1)], "w_arr", "w_out")
+    need(v, "r_tmp")
+    inc(v.tensor_copy(T.r[:, 8 * rank:8 * rank + 8], T.rtmp[:, 0:8]), "r_own")
     ts("c_dg", T.diag[:, :], T.rowi[:, 0:16], T.cf[:, :], Op.is_equal)
-
-    need(v, "ld_tid")
-    ts("s_th", T.thi[:, :], T.ti[:, :], 8, Op.arith_shift_right)
-    ts("s_th", T.tlo[:, :], T.ti[:, :], 255, Op.bitwise_and)
-    ts("s_th", T.tz[:, :], T.ti[:, :], 0.0, Op.is_equal, -65536.0, Op.mult)
-    need(v, "s_th")
-    inc(v.tensor_tensor(T.hi[:, :], T.thi[:, :], T.tz[:, :], Op.add), "s_id")
-    inc(v.tensor_copy(T.lo[:, :], T.tlo[:, :]), "s_id")
-    need(g, "s_id")
-    spread([(T.hi[:, :], T.idh[rank]), (T.lo[:, :], T.idl[rank])], "id_arr", "id_out")
 
     def wrap(src, col, done, based, after):
         o = T.pb4[:, col:col + 48] if based else T.pb6[:, 0:48]
@@ -162,8 +183,14 @@ def rank_program(g, core, T, topo):
 
     need(pe, "c_sel")
     wrap(T.bm, 0, "p_base", False, "b_mul")
-    need(act, "p_base")
-    inc(act.activation(T.baseb[:, :], T.pb6[:, 0:48], Act.Copy), "b_base")
+    need(v, "p_base")
+    inc(v.tensor_copy(T.letl[:, :], T.pb6[:, 0:48]), "l_l")
+    inc(v.tensor_copy(T.ln[:, :], T.pb6[:, 0:48]), "l_n")
+    need(v, "l_n")
+    ts("l_q", T.lq[:, :], T.ln[:, :], 3, Op.arith_shift_right)
+    need(v, "l_q")
+    ts("b_base", T.baseb[:, :], T.lq[:, :], 512.0, Op.mult, 256.0, Op.add)
+    ts("l_k", T.lk[:, :], T.lq[:, :], -4.0, Op.mult)
 
     cn = MW * ((rank + 1) % n)
     need(pe, "sm_arr")
@@ -171,25 +198,26 @@ def rank_program(g, core, T, topo):
     for q in range(n):
         call = pe.matmul(T.pb5[:, 8:24], T.gb[0:8, :], T.sm[0:8, MW * q:MW * q + 16], q == 0, q == n - 1)
     inc(call, "p_halo")
-    need(v, "p_halo", "c_dg")
-    inc(v.tensor_tensor(T.rd[:, :], T.pb5[:, 8:24], T.diag[:, :], Op.mult), "r_diag")
-    need(v, "r_diag")
-    inc(v.tensor_reduce(T.rootc[:, :], T.rd[:, :], AxisListType.X, Op.add), "r_col")
-    need(v, "r_col", "e_main")
-    ts("r_mul", T.rm[:, :], T.e[:, 0:S], T.rootc[:, :], Op.mult)
+    need(v, "l_k", "p_halo", "c_dg")
     ts("e_halo", T.e[:, S:S + 4], T.pb5[:, 0:4], T.cf[:, :], Op.is_equal)
+    inc(v.tensor_tensor(T.lc[:, :], T.ln[:, :], T.lk[:, :], Op.add), "l_c")
+    inc(v.tensor_tensor(T.rd[:, :], T.pb5[:, 8:24], T.diag[:, :], Op.mult), "r_diag")
+    need(v, "r_diag", "l_c")
+    inc(v.tensor_reduce(T.rootc[:, :], T.rd[:, :], AxisListType.X, Op.add), "r_col")
+    inc(v.tensor_copy(T.letc[:, :], T.lc[:, :]), "l_cc")
+    need(v, "r_col")
+    ts("r_all", T.rall[:, 0:1], T.rootc[:, :], T.basec[:, :], Op.add)
 
-    for queue, row, own, land in ((sp, 0, T.hi, T.idh), (act, 1, T.lo, T.idl)):
-        need(queue, "z_w2", "s_id", "id_arr")
+    for queue, row, own in ((sp, 0, T.hi), (act, 1, T.lo)):
+        need(queue, "z_w2", "s_sm")
         inc(queue.dma_start(T.v[row:128:16, cw:cw + M], own[:, :]), "w2_in", 16)
+    for queue, row, land in ((sp, 0, T.idh), (act, 1, T.idl)):
+        need(queue, "sm_arr")
         for j in range(1, n):
             q = (rank + j) % n
             inc(queue.dma_start(T.v[row:128:16, M * q:M * q + M], land[q]), "w2_in", 16)
-    need(pe, "b_base")
-    wrap(T.rm, 0, "p_list1", True, "r_mul")
 
     win, win2 = T.w[:, 0:4 * M], T.v[:, 0:4 * M]
-    need(v, "e_halo", "w_own")
     zb = {1: T.pb5, 2: T.pb6, 3: T.pb7, 4: T.pb0, 5: T.pb1}
 
     def keep(k):
@@ -218,12 +246,28 @@ def rank_program(g, core, T, topo):
 
     for k in range(1, 6):
         lst, a = T["list%d" % k], T["a%d" % k]
+        if k == 1:
+            need(v, "l_l", "r_own", "r_arr", "e_halo", "e_main")
+            inc(v.tensor_tensor(T.m1[:, :], T.r[:, 0:32].indirect(T.letl[:, 0:48]), T.e[:, 1:1 + S], Op.mult), "v_m1")
+            need(pe, "b_base")
+            wrap(T.m1, 48, "p_list2", True, "v_m1")
+            need(act, "w2_in", "r_all", "l_cc")
+            inc(act.activation(T.rid[:, :], win2.indirect(T.rall[:, 0:1]), Act.Copy), "a_rid")
+            need(act, "a_rid")
+            inc(act.activation(a[:, :], T.rid[:, 0:16].indirect(T.letc[:, 0:48]), Act.Copy), "a_id1")
+            ts("c_w", T.wz[:, :], T.cf[:, :], 0.0, Op.is_equal, 256.0, Op.mult)
+            ts("c_w", T.wy[:, :], T.cf[:, :], 1.0, Op.is_equal)
+            ts("c_idf", T.idf[:, :], T.rowi[:, :], T.pf[:, :], Op.is_equal)
+            need(v, "c_w")
+            inc(v.tensor_tensor(T.wc[:, :], T.wz[:, :], T.wy[:, :], Op.add), "c_wc")
+            need(v, "c_wc")
+            ts("c_wg", T.wg[:, :], T.grp[:, :], T.wc[:, :], Op.mult)
+            continue
         need(v, "p_list%d" % k)
         inc(v.tensor_copy(lst[:, :], T.pb4[:, 48 * (k - 1):48 * k]), "v_list%d" % k)
         need(v, "v_list%d" % k)
         need(act, "v_list%d" % k)
-        if k == 1:
-            need(act, "w2_in")
+        if k == 2:
             need(v, "w_arr")
         if k < 5:
             mk = T["m%d" % k]
@@ -231,26 +275,20 @@ def rank_program(g, core, T, topo):
             inc(act.activation(a[:, :], win2.indirect(lst[:, 0:48]), Act.Copy), "a_id%d" % k)
             need(pe, "v_list%d" % k)
             wrap(mk, 48 * k, "p_list%d" % (k + 1), True, "v_m%d" % k)
-            if k == 1:
-                ts("c_w", T.wz[:, :], T.cf[:, :], 0.0, Op.is_equal, 256.0, Op.mult)
-                ts("c_w", T.wy[:, :], T.cf[:, :], 1.0, Op.is_equal)
-                ts("c_idf", T.idf[:, :], T.rowi[:, :], T.pf[:, :], Op.is_equal)
-                need(v, "c_w")
-                inc(v.tensor_tensor(T.wc[:, :], T.wz[:, :], T.wy[:, :], Op.add), "c_wc")
-                need(v, "c_wc")
-                ts("c_wg", T.wg[:, :], T.grp[:, :], T.wc[:, :], Op.mult)
+            if k == 2:
+                ids(1)
             if k == 3:
-                ids(1, 2)
-            if k == 4:
+                ids(2, 3)
                 keep(1)
+            if k == 4:
                 keep(2)
-                ids(3, 4)
+                keep(3)
+                ids(4)
         else:
             need(v, "w2_in")
             inc(v.tensor_copy(a[:, 0:384], win2.indirect(lst[:, 0:24])), "a_id5")
             inc(act.activation(a[:, 384:768], win2.indirect(lst[:, 24:48]), Act.Copy), "a_id6")
             ids(5)
-            keep(3)
             keep(4)
     keep(5)
 
@@ -268,4 +306,4 @@ def rank_program(g, core, T, topo):
     inc(sp.dma_start(T.yid[:, :], T.yi[0:48, :]), "st_id", 16)
     need(act, "st_len")
     need(sp, "st_id")
-    need(g, "sm_out", "w_out", "id_out")
+    need(g, "sm_out", "w_out", "r_out")

@@ -2,17 +2,18 @@ from concourse.bass import DstId, RemoteDMATransfer
 from concourse.mybir import AluOpType as Op, ActivationFunctionType as Act, AxisListType
 
 S, M = 768, 512
-MW = 32
+H = S // 2
+MW = 16
+R = 80
 C = 131072.0
 BIG = 1.5 * 2.0 ** 40
 SCRATCH = {"x": ("sbuf", [128, 4, 8, 16], "int32"), "xb": ("sbuf", [128, 8, 4, 16], "bfloat16"),
-           "idh": ("dram", [4, 128, 32], "bfloat16"), "idl": ("dram", [4, 128, 32], "bfloat16")}
-for _t, _s in (("int32", "li768 ti32 thi32 tlo32 rt16 pi1 gi1 ci1 oi1 rowi128 rowg128 ln48 lq48 lk48 lc48"),
-               ("float32", "tz32 rd16 diag16 dgown16 rx16 pf1 gf1 cf1 cown1 ncf1 wz1 wy1 wc1 basec1 lcol1 oix1 rootc1 roott1 "
-                           "idf128 grp8 d48 rr128 yl128 yi128"),
-               ("uint16", "rown2 rall2 letl48 letc48"),
-               ("bfloat16", "l768 hi32 lo32 sm128 w2048 v2048 ab768 e784 bm768 sel2048 ones16 gb128 idb128 wg8 baseb48 "
-                            "rtmp16 r32 rid16")):
+           "ido": ("dram", [128, 64], "bfloat16"), "idr": ("dram", [4, 128, 64], "bfloat16")}
+for _t, _s in (("int32", "li192 ti64 thi64 tlo64 rw1 pi1 ci1 oi1 rowi128 rowq128 ln48 lq48"),
+               ("float32", "tz64 pf1 gf1 cf1 ncf1 ncg1 wz1 wx1 wy1 wc1 basec1 rootc1 grp8 rr128 yl128 yi128"),
+               ("uint16", "rown2 rall2 lown4 rl20 letl48 letc48"),
+               ("bfloat16", "l192 hi64 lo64 sm64 w2048 v2048 ab768 e784 bm784 sel2048 ones128 neg48 gbs512 idb128 wg288 baseb48 "
+                            "sb48 r320 rid16 ridb320")):
     for _n in _s.split():
         _b = _n.rstrip("0123456789")
         SCRATCH[_b] = ("sbuf", [128, int(_n[len(_b):])], _t)
@@ -20,16 +21,16 @@ for _k in range(1, 6):
     SCRATCH["list%d" % _k] = ("sbuf", [128, 48], "uint16")
     SCRATCH["a%d" % _k] = ("sbuf", [128, S], "bfloat16")
     SCRATCH["m%d" % _k] = ("sbuf", [128, S], "bfloat16")
-    SCRATCH["t%d" % _k] = ("sbuf", [128, 48], "float32")
-    SCRATCH["d%dm" % _k] = ("sbuf", [128, 48], "float32")
+    SCRATCH["d%dm" % _k] = ("sbuf", [128, 128], "float32")
 for _k in range(8):
     SCRATCH["pb%d" % _k] = ("psum", [128, 512], "float32")
-SEMAPHORES = ("ld_lett ld_tid ld_root ld_kid sm_arr w_arr r_arr sm_out w_out r_out w2_in st_id st_len iota z_w2 z_sel z_ones "
-              "z_sm c_a c_b c_f c_lc c_dg c_do c_gb c_id c_idf c_grp c_w c_wc c_wg c_sel s_th s_sm s_l0 s_l1 p_l0 p_l1 p_own o_rx "
-              "o_rt o_ls x_conv0 x_conv1 p_x0 p_x1 w_own r_tmp r_own e_abs e_main b_mul p_base l_n l_l l_q l_k l_c l_cc b_base "
-              "p_halo e_halo r_diag r_col r_all a_rid rr_ok p_t yi_ok yl_ok d_5 a_id6").split()
+SEMAPHORES = ("ld_lett ld_tid ld_root ld_kid sm_arr w_arr r_arr sm_out w_out r_out w2_in st_id st_len iota z_w2 z_w3 z_sel z_sel2 "
+              "z_ones z_sm z_rl c_a c_b c_gs c_id c_grp c_bc c_w c_wx c_wc c_wg c_sel s_th s_id s_sm id_st id_arr id_out s_l "
+              "p_l0 p_l1 o_ls o_l2 w_own r_tmp r_own e_abs e_main b_mul b_h p_halo e_halo r_col r_all p_c1 p_c2 l_n l_cc l_q l_s "
+              "b_base l_l r_l a_rid a_ridb rr_ok yi_ok yl_ok x_conv0 x_conv1 p_x0 p_x1 p_x2 p_x3 v_id5a v_id5b c_gf z_wg").split()
 for _k in range(1, 6):
-    SEMAPHORES += [_n % _k for _n in ("p_list%d", "v_list%d", "v_m%d", "a_id%d", "p_z%d", "v_t%d", "v_d%d")]
+    SEMAPHORES += [_n % _k for _n in ("p_z%d", "v_d%d", "a_id%d", "b_id%d", "v_m%da", "v_m%db", "p_list%da", "p_list%db",
+                                      "v_list%da", "v_list%db")]
 
 
 def rank_program(g, core, T, topo):
@@ -57,247 +58,284 @@ def rank_program(g, core, T, topo):
     near_e = [e for e in range(16) if all(e in topo.engines(core, d) for d in near) and e not in far_e]
     near_e = near_e[:len(far_e) * len(near) // len(far)]
 
-    def spread(pieces, arr, out):
+    def spread(src, dst, arr, out):
         tr = []
         for ds, es in ((far, far_e), (near, near_e)):
             ids = []
             for d in ds:
                 rid, pid = topo.addr(d, core)
                 ids.append(DstId(rid=rid, pnc=pid))
-            at = 0
-            for src, dst, share in pieces:
-                w = len(es) // share
-                tr.append(RemoteDMATransfer(dst_ids=ids, dma_engine_mask=sum(1 << e for e in es[at:at + w]),
-                                            remote_sem=T.sem[arr], srcs=[src], dsts=[dst for _ in ds]))
-                at += w
-            count[out] = count.get(out, 0) + at
-            count[arr] = count.get(arr, 0) + at * len(ds)
+            tr.append(RemoteDMATransfer(dst_ids=ids, dma_engine_mask=sum(1 << e for e in es),
+                                        remote_sem=T.sem[arr], srcs=[src], dsts=[dst for _ in ds]))
+            count[out] = count.get(out, 0) + len(es)
+            count[arr] = count.get(arr, 0) + len(es) * len(ds)
         g.remote_dma_fused(tr, local_sem=T.sem[out])
 
-    c0, cw, o = MW * rank, M * rank, 4 * rank
-    inc(act.dma_start(T.rt[0:8, :], T.kid[:, 16:32]), "ld_root", 16)
-    inc(sp.dma_start(T.li[0:8, :], T.lett[:, :]), "ld_lett", 16)
-    inc(sp.dma_start(T.ti[:, :], T.tid[:, :]), "ld_tid", 16)
+    c0, cw, r0, o = MW * rank, M * rank, R * rank, 4 * rank
+    inc(act.dma_start(T.rw[:, 0:1], T.kid[:, 16:32]), "ld_root", 16)
+    inc(sp.dma_start(T.li[0:32, :], T.lett[:, :]), "ld_lett", 16)
+    inc(sp.dma_start(T.ti[0:64, :], T.tid[:, :]), "ld_tid", 16)
     for q4 in range(4):
-        for a, queue in ((0, sp), (1, act)):
-            h = 4 * a + q4
-            inc(queue.dma_start(T.x[64 * a:64 * a + 64, q4, :, :], T.kid[h:h + 1, :]), "ld_kid", 16)
+        inc((sp, act)[q4 % 2].dma_start(T.x[:, q4, :, :], T.kid[q4:8:4, :]), "ld_kid", 16)
 
     inc(g.iota(T.pi[:, :], [[0, 1]], 0, 1), "iota")
     inc(g.iota(T.rowi[:, :], [[1, 128]], 0, 0), "iota")
-    inc(v.memset(T.sel[:, :], 0.0), "z_sel")
+    inc(g.iota(T.v[:, 1024:2048], [[0, 1024]], 0, 0, allow_small_or_imprecise_dtypes=True), "z_w3")
+    inc(v.memset(T.sel[:, 0:1024], 0.0), "z_sel")
     inc(v.memset(T.sm[:, c0:c0 + MW], 0.0), "z_sm")
     inc(v.memset(T.ones[:, :], 1.0), "z_ones")
-    need(act, "z_sel")
-    inc(act.activation(T.v[:, :], T.sel[:, :], Act.Copy), "z_w2")
+    inc(v.memset(T.neg[:, :], -C), "z_ones")
     need(v, "iota")
-    ts("c_a", T.gi[:, :], T.pi[:, :], 4, Op.arith_shift_right)
     ts("c_a", T.ci[:, :], T.pi[:, :], 15, Op.bitwise_and)
-    ts("c_a", T.rowg[:, :], T.rowi[:, :], 4, Op.arith_shift_right)
+    ts("c_a", T.rowq[:, :], T.rowi[:, :], 2, Op.arith_shift_right, 28, Op.bitwise_and)
     inc(v.tensor_copy(T.pf[:, :], T.pi[:, :]), "c_a")
     need(v, "c_a")
-    inc(v.tensor_copy(T.gf[:, :], T.gi[:, :]), "c_b")
-    inc(v.tensor_copy(T.cf[:, :], T.ci[:, :]), "c_b")
     ts("c_b", T.ncf[:, :], T.ci[:, :], -1.0, Op.mult)
-    ts("c_b", T.cown[:, :], T.ci[:, :], float(o), Op.add)
-    ts("c_b", T.oi[:, :], T.ci[:, :], 2, Op.arith_shift_right)
-    ts("c_gb", T.gb[0:8, :], T.rowg[0:8, :], T.pf[0:8, :], Op.is_equal)
+    inc(v.tensor_copy(T.cf[:, :], T.ci[:, :]), "c_b")
+    for s in range(4):
+        ts("c_gs", T.gbs[0:32, 128 * s:128 * s + 128], T.rowq[0:32, :], float(s), Op.add, T.pf[0:32, :], Op.is_equal)
     ts("c_id", T.idb[:, :], T.rowi[:, :], T.pf[:, :], Op.is_equal)
+    need(act, "z_sel")
+    inc(act.activation(T.sel[:, 1024:2048], T.sel[:, 0:1024], Act.Copy), "z_sel2")
+    inc(act.activation(T.v[:, 0:1024], T.sel[:, 0:1024], Act.Copy), "z_w2")
+    inc(act.activation(T.wg[:, :], T.sel[:, 0:288], Act.Copy), "z_wg")
+    need(act, "c_a", "c_b")
+    inc(act.activation(T.ncg[:, :], T.ncf[:, :], Act.Copy, scale=0.0625), "c_bc")
+    inc(act.activation(T.wz[:, :], T.cf[:, :], Act.Relu, bias=1.0, scale=-1.0), "c_w")
+    inc(act.activation(T.wx[:, :], T.cf[:, :], Act.Abs, bias=T.neg1[:, :]) if False else
+        act.activation(T.wx[:, :], T.cf[:, :], Act.Square, bias=-1.0), "c_wx")
+    need(act, "c_bc")
+    inc(act.activation(T.gf[:, :], T.pf[:, :], Act.Identity, bias=T.ncg[:, :], scale=0.0625), "c_gf")
+    need(act, "c_wx")
+    inc(act.activation(T.wy[:, :], T.wx[:, :], Act.Relu, bias=1.0, scale=-1.0), "c_w")
+    need(act, "c_w")
+    inc(act.activation(T.wc[:, :], T.wz[:, :], Act.Identity, bias=T.wy[:, :], scale=256.0), "c_wc")
 
-    need(v, "ld_root", "z_sm")
-    ts("s_sm", T.sm[0:8, c0 + o:c0 + o + 4], T.rt[0:8, o:o + 4], -256.0, Op.add)
-    need(v, "ld_lett")
-    inc(v.tensor_copy(T.sm[0:8, c0 + 16:c0 + 20], T.li[0:8, 0:4]), "s_sm")
+    need(v, "ld_lett", "z_sm")
+    inc(v.tensor_copy(T.l[0:32, :], T.li[0:32, :]), "s_l")
     need(v, "ld_tid")
-    ts("s_th", T.thi[:, :], T.ti[:, :], 8, Op.arith_shift_right)
-    ts("s_th", T.tlo[:, :], T.ti[:, :], 255, Op.bitwise_and)
-    ts("s_th", T.tz[:, :], T.ti[:, :], 0.0, Op.is_equal, -65536.0, Op.mult)
-    need(v, "s_th")
-    inc(v.tensor_tensor(T.hi[:, :], T.thi[:, :], T.tz[:, :], Op.add), "s_sm")
-    inc(v.tensor_copy(T.lo[:, :], T.tlo[:, :]), "s_sm")
+    i64 = slice(0, 64)
+    ts("s_th", T.thi[i64, :], T.ti[i64, :], 8, Op.arith_shift_right)
+    ts("s_th", T.tlo[i64, :], T.ti[i64, :], 255, Op.bitwise_and)
+    ts("s_th", T.tz[i64, :], T.ti[i64, :], 0.0, Op.is_equal, -65536.0, Op.mult)
+    inc(v.tensor_copy(T.sm[0:32, c0 + 8:c0 + 12], T.li[0:32, 0:4]), "s_sm")
+    need(v, "ld_root", "s_th")
+    inc(v.tensor_tensor(T.hi[i64, :], T.thi[i64, :], T.tz[i64, :], Op.add), "s_id")
+    inc(v.tensor_copy(T.lo[i64, :], T.tlo[i64, :]), "s_id")
+    ts("s_sm", T.sm[:, c0:c0 + 1], T.rw[:, 0:1], -256.0, Op.add)
+    inc(v.tensor_copy(T.rown[:, 0:1], T.rw[:, 0:1]), "o_ls")
     need(g, "s_sm")
-    spread([(T.sm[:, c0:c0 + MW], T.sm[:, c0:c0 + MW], 2), (T.hi[:, :], T.idh[rank], 4), (T.lo[:, :], T.idl[rank], 4)],
-           "sm_arr", "sm_out")
-    need(pe, "s_sm", "c_gb")
-    inc(pe.matmul(T.pb7[:, 0:16], T.gb[0:8, :], T.sm[0:8, c0:c0 + 16], True, True), "p_own")
-    for j in range(2):
-        inc(v.tensor_copy(T.l[0:8, 384 * j:384 * j + 384], T.li[0:8, 384 * j:384 * j + 384]), "s_l%d" % j)
-        need(pe, "s_l%d" % j)
-        inc(pe.matmul(T["pb%d" % j][:, 0:384], T.gb[0:8, :], T.l[0:8, 384 * j:384 * j + 384], True, True), "p_l%d" % j)
-    need(v, "c_b")
-    ts("c_do", T.dgown[:, :], T.rowi[:, 0:16], T.cown[:, :], Op.is_equal)
-    ts("c_f", T.basec[:, :], T.oi[:, :], 512.0, Op.mult, 256.0, Op.add)
-    ts("c_f", T.oix[:, :], T.oi[:, :], 4.0, Op.mult)
-    need(v, "c_do", "c_f", "p_own")
-    inc(v.tensor_tensor(T.rx[:, :], T.pb7[:, 0:16], T.dgown[:, :], Op.mult), "o_rx")
-    inc(v.tensor_tensor(T.lcol[:, :], T.oix[:, :], T.cf[:, :], Op.add), "c_lc")
-    ts("c_grp", T.grp[:, :], T.rowi[:, 0:8], T.gf[:, :], Op.is_equal)
-    need(v, "o_rx")
-    inc(v.tensor_reduce(T.roott[:, :], T.rx[:, :], AxisListType.X, Op.add), "o_rt")
-    need(v, "o_rt")
-    ts("o_ls", T.rown[:, 0:1], T.roott[:, :], 256.0, Op.add)
-
-    need(act, "c_b")
+    spread(T.sm[:, c0:c0 + MW], T.sm[:, c0:c0 + MW], "sm_arr", "sm_out")
+    need(sp, "s_id")
+    inc(sp.dma_start(T.ido[0:64, :], T.hi[i64, :]), "id_st", 16)
+    inc(sp.dma_start(T.ido[64:128, :], T.lo[i64, :]), "id_st", 16)
+    need(g, "id_st")
+    spread(T.ido[:, :], T.idr[rank], "id_arr", "id_out")
+    need(pe, "s_l", "c_gs")
+    for s in range(4):
+        inc(pe.matmul(T["pb%d" % (s // 2)][:, 192 * (s % 2):192 * (s % 2) + 192], T.gbs[0:32, 128 * s:128 * s + 128],
+                      T.l[0:32, :], True, True), "p_l%d" % (s // 2))
     for j in range(2):
         need(act, "p_l%d" % j)
-        inc(act.activation(T.ab[:, 384 * j:384 * j + 384], T["pb%d" % j][:, 0:384], Act.Abs, bias=T.ncf[:, :]), "e_abs")
-    need(act, "e_abs")
-    inc(act.activation(T.e[:, 0:S], T.ab[:, :], Act.Relu, bias=1.0, scale=-1.0), "e_main")
-    need(act, "e_main", "c_lc")
-    inc(act.activation(T.bm[:, :], T.e[:, 0:S], Act.Copy, scale=T.lcol[:, :]), "b_mul")
+        inc(act.activation(T.ab[:, H * j:H * j + H], T["pb%d" % j][:, 0:H], Act.Abs, bias=T.ncf[:, :]), "e_abs")
 
     need(v, "ld_kid")
     for par in range(2):
         for q4 in range(4):
             ts("x_conv%d" % par, T.xb[:, par:8:2, q4, :], T.x[:, q4, par:8:2, :], -256.0, Op.add)
     need(pe, "c_id")
-    need(v, "c_grp", "z_sel", "z_ones", "z_w2")
-    for par in range(2):
-        need(pe, "x_conv%d" % par)
-        for ml in range(par, 8, 2):
+    xbank = [T.pb2, T.pb3, T.pb4, T.pb6]
+    for u in (0, 2, 1, 3):
+        need(pe, "x_conv%d" % (u % 2))
+        for j in range(2):
             for a in range(2):
                 p = slice(64 * a, 64 * a + 64)
-                inc(pe.matmul(T["pb%d" % (2 + par)][p, ml // 2:256:4], T.xb[p, ml, :, :], T.idb[p, p], True, True), "p_x%d" % par)
-        for h in range(4 * par, 4 * par + 4):
-            ts("c_sel", T.sel[:, 16 * h:2048:129], T.ones[:, :], T.grp[:, h:h + 1], Op.mult)
-        need(v, "p_x%d" % par)
-        inc(v.tensor_copy(T.w[:, cw + par:cw + M:2], T["pb%d" % (2 + par)][:, 0:256]), "w_own")
+                inc(pe.matmul(xbank[u][p, j:128:2], T.xb[p, u + 4 * j, :, :], T.idb[p, p], True, True), "p_x%d" % u)
+    for u in (0, 2, 1, 3):
+        queue = (act, v)[u % 2]
+        need(queue, "p_x%d" % u)
+        land, bank = T.w[:, cw + u:cw + M:4], xbank[u][:, 0:128]
+        inc(act.activation(land, bank, Act.Copy) if u % 2 == 0 else v.tensor_copy(land, bank), "w_own")
     need(v, "w_own", "o_ls")
-    inc(v.tensor_copy(T.rtmp[:, :], T.w[:, cw:cw + M].indirect(T.rown[:, 0:1])), "r_tmp")
-    need(g, "r_tmp")
-    spread([(T.rtmp[:, 0:8], T.r[:, 8 * rank:8 * rank + 8], 1)], "r_arr", "r_out")
-    need(g, "w_own")
-    spread([(T.w[:, cw:cw + M], T.w[:, cw:cw + M], 1)], "w_arr", "w_out")
+    inc(v.tensor_copy(T.r[:, r0 + 64:r0 + 80], T.w[:, cw:cw + M].indirect(T.rown[:, 0:1])), "r_tmp")
     need(v, "r_tmp")
-    inc(v.tensor_copy(T.r[:, 8 * rank:8 * rank + 8], T.rtmp[:, 0:8]), "r_own")
-    ts("c_dg", T.diag[:, :], T.rowi[:, 0:16], T.cf[:, :], Op.is_equal)
+    ts("o_l2", T.lown[:, 0:4], T.r[:, r0 + 64 + o:r0 + 68 + o], 256.0, Op.add)
+    need(v, "o_l2")
+    inc(v.tensor_copy(T.r[:, r0:r0 + 64], T.w[:, cw:cw + M].indirect(T.lown[:, 0:4])), "r_own")
+    need(g, "r_tmp", "r_own")
+    spread(T.r[:, r0:r0 + R], T.r[:, r0:r0 + R], "r_arr", "r_out")
+    need(g, "w_own")
+    spread(T.w[:, cw:cw + M], T.w[:, cw:cw + M], "w_arr", "w_out")
 
-    def wrap(src, col, done, based, after):
-        o = T.pb4[:, col:col + 48] if based else T.pb6[:, 0:48]
-        if based:
-            pe.matmul(o, T.idb[:, :], T.baseb[:, :], True, False)
-        need(pe, after)
-        for i in range(16):
-            call = pe.matmul(o, T.sel[:, 128 * i:128 * i + 128], src[:, i:S:16], i == 0 and not based, i == 15)
-        inc(call, done)
+    need(v, "c_gf")
+    ts("c_grp", T.grp[:, :], T.rowi[:, 0:8], T.gf[:, :], Op.is_equal)
+    need(v, "c_grp", "z_sel", "z_sel2", "z_w2", "z_wg", "z_ones")
+    for h in range(8):
+        ts("c_sel", T.sel[:, 16 * h:2048:129], T.ones[:, 0:16], T.grp[:, h:h + 1], Op.mult)
 
-    need(pe, "c_sel")
-    wrap(T.bm, 0, "p_base", False, "b_mul")
-    need(v, "p_base")
-    inc(v.tensor_copy(T.letl[:, :], T.pb6[:, 0:48]), "l_l")
-    inc(v.tensor_copy(T.ln[:, :], T.pb6[:, 0:48]), "l_n")
-    need(v, "l_n")
-    ts("l_q", T.lq[:, :], T.ln[:, :], 3, Op.arith_shift_right)
-    need(v, "l_q")
-    ts("b_base", T.baseb[:, :], T.lq[:, :], 512.0, Op.mult, 256.0, Op.add)
-    ts("l_k", T.lk[:, :], T.lq[:, :], -4.0, Op.mult)
+    need(act, "e_abs")
+    inc(act.activation(T.e[:, 0:S], T.ab[:, :], Act.Relu, bias=1.0, scale=-1.0), "e_main")
+    need(act, "e_main")
+    inc(act.activation(T.bm[:, 0:S], T.e[:, 0:S], Act.Copy, scale=T.cf[:, :]), "b_mul")
+    need(act, "c_wc", "z_wg", "c_grp")
+    for b in range(6):
+        inc(act.activation(T.wg[:, 48 * b + b:48 * b + 48:6], T.grp[:, :], Act.Copy, scale=T.wc[:, :]), "c_wg")
 
     cn = MW * ((rank + 1) % n)
-    need(pe, "sm_arr")
-    inc(pe.matmul(T.pb5[:, 0:4], T.gb[0:8, :], T.sm[0:8, cn + 16:cn + 20], True, True), "p_halo")
-    for q in range(n):
-        call = pe.matmul(T.pb5[:, 8:24], T.gb[0:8, :], T.sm[0:8, MW * q:MW * q + 16], q == 0, q == n - 1)
-    inc(call, "p_halo")
-    need(v, "l_k", "p_halo", "c_dg")
+    need(pe, "s_sm", "sm_arr")
+    inc(pe.matmul(T.pb5[:, 0:4], T.gbs[0:32, 0:128], T.sm[0:32, cn + 8:cn + 12], True, True), "p_halo")
+    need(v, "p_halo", "c_b")
+    ts("b_h", T.bm[:, S:S + 1], T.pb5[:, 0:1], T.cf[:, :], Op.is_equal, T.cf[:, :], Op.mult)
     ts("e_halo", T.e[:, S:S + 4], T.pb5[:, 0:4], T.cf[:, :], Op.is_equal)
-    inc(v.tensor_tensor(T.lc[:, :], T.ln[:, :], T.lk[:, :], Op.add), "l_c")
-    inc(v.tensor_tensor(T.rd[:, :], T.pb5[:, 8:24], T.diag[:, :], Op.mult), "r_diag")
-    need(v, "r_diag", "l_c")
-    inc(v.tensor_reduce(T.rootc[:, :], T.rd[:, :], AxisListType.X, Op.add), "r_col")
-    inc(v.tensor_copy(T.letc[:, :], T.lc[:, :]), "l_cc")
+
+    need(pe, "c_sel", "b_mul")
+    for i in range(16):
+        call = pe.matmul(T.pb6[:, 0:48], T.sel[:, 128 * i:128 * i + 128], T.bm[:, i:i + 753:16], i == 0, i == 15)
+    inc(call, "p_c1")
+    for i in range(16):
+        if i == 15:
+            need(pe, "b_h")
+        pe.matmul(T.pb7[:, 0:48], T.sel[:, 128 * i:128 * i + 128], T.bm[:, i + 1:i + 754:16], i == 0, False)
+    need(v, "p_c1")
+    ts("l_n", T.ln[:, :], T.pb6[:, 0:48], 16.0, Op.mult)
+    need(v, "l_n")
+    ts("l_q", T.lq[:, :], T.ln[:, :], 2, Op.arith_shift_right, 48, Op.bitwise_and)
+    inc(v.tensor_copy(T.letc[:, :], T.pb6[:, 0:48]), "l_cc")
+    need(v, "l_q")
+    inc(v.tensor_tensor(T.sb[:, :], T.ln[:, :], T.lq[:, :], Op.add), "l_s")
+    ts("b_base", T.baseb[:, :], T.lq[:, :], 32.0, Op.mult, 256.0, Op.add)
+    need(pe, "l_s")
+    inc(pe.matmul(T.pb7[:, 0:48], T.idb[:, :], T.sb[:, :], False, True), "p_c2")
+    need(v, "p_c2")
+    inc(v.tensor_copy(T.letl[:, :], T.pb7[:, 0:48]), "l_l")
+    ts("c_a", T.oi[:, :], T.ci[:, :], 2, Op.arith_shift_right)
+    inc(v.memset(T.rl[:, :], 0), "z_rl")
+    need(v, "sm_arr", "s_sm")
+    inc(v.tensor_reduce(T.rootc[:, :], T.sm[:, 0:MW * n:MW], AxisListType.X, Op.add), "r_col")
+    need(v, "c_a")
+    ts("r_col", T.basec[:, :], T.oi[:, :], 512.0, Op.mult, 1024.0, Op.add)
     need(v, "r_col")
     ts("r_all", T.rall[:, 0:1], T.rootc[:, :], T.basec[:, :], Op.add)
 
-    for queue, row, own in ((sp, 0, T.hi), (act, 1, T.lo)):
-        need(queue, "z_w2", "s_sm")
-        inc(queue.dma_start(T.v[row:128:16, cw:cw + M], own[:, :]), "w2_in", 16)
-    for queue, row, land in ((sp, 0, T.idh), (act, 1, T.idl)):
-        need(queue, "sm_arr")
-        for j in range(1, n):
-            q = (rank + j) % n
-            inc(queue.dma_start(T.v[row:128:16, M * q:M * q + M], land[q]), "w2_in", 16)
+    for j in range(n):
+        q = (rank + j) % n
+        for queue, row, half in ((sp, 0, slice(0, 64)), (act, 1, slice(64, 128))):
+            need(queue, "id_arr" if j else "id_st")
+            if j == 0:
+                need(queue, "z_w2", "z_w3")
+            inc(queue.dma_start(T.v[row:128:16, M * q:M * q + M], T.idr[q, half, :] if j else T.ido[half, :]), "w2_in", 16)
 
     win, win2 = T.w[:, 0:4 * M], T.v[:, 0:4 * M]
-    zb = {1: T.pb5, 2: T.pb6, 3: T.pb7, 4: T.pb0, 5: T.pb1}
+    zb = {1: T.pb0, 2: T.pb5, 3: T.pb6, 4: T.pb7, 5: T.pb1}
+    lbank = {"a": T.pb4, "b": T.pb2}
+    part = {"a": 0, "b": 1}
+
+    def step(k, f):
+        h = part[f]
+        src = T.r[:, 0:4 * R].indirect(T.letl[:, 24 * h:24 * h + 24]) if k == 2 else \
+            win.indirect(T["list%d" % k][:, 24 * h:24 * h + 24])
+        inc(v.tensor_tensor(T["m%d" % k][:, H * h:H * h + H], src, T.e[:, k + H * h:k + H * h + H], Op.mult), "v_m%d%s" % (k, f))
+
+    def wrap(k, f):
+        h = part[f]
+        if k > 2:
+            need(pe, "v_list%d%s" % (k, f))
+        out = lbank[f][:, 32 * (k - 2):32 * (k - 2) + 24]
+        pe.matmul(out, T.idb[:, :], T.baseb[:, 24 * h:24 * h + 24], True, False)
+        need(pe, "v_m%d%s" % (k, f))
+        for i in range(16):
+            call = pe.matmul(out, T.sel[:, 128 * i:128 * i + 128], T["m%d" % k][:, H * h + i:H * h + H:16], False, i == 15)
+        inc(call, "p_list%d%s" % (k + 1, f))
+
+    def take(k, f):
+        h = part[f]
+        need(v, "p_list%d%s" % (k, f))
+        inc(v.tensor_copy(T["list%d" % k][:, 24 * h:24 * h + 24], lbank[f][:, 32 * (k - 3):32 * (k - 3) + 24]),
+            "v_list%d%s" % (k, f))
+        need(v, "v_list%d%s" % (k, f))
+
+    def ids(k):
+        z = zb[k][0:48, 0:128]
+        pe.matmul(z, T.neg[0:5 - k, 0:48], T.ones[0:5 - k, :], True, False)
+        need(pe, "a_id%d" % k)
+        for b in range(6):
+            call = pe.matmul(z, T.wg[:, 48 * b:48 * b + 48], T["a%d" % k][:, 128 * b:128 * b + 128], False, b == 5)
+        inc(call, "p_z%d" % k)
 
     def keep(k):
         need(v, "p_z%d" % k)
+        z, d = zb[k][0:48, 0:128], T["d%dm" % k][0:48, :]
         if k == 1:
-            ts("v_d1", T.d1m[:, :], zb[1][:, 0:48], -C, Op.max, -C, Op.add)
+            ts("v_d1", d, z, -5.0 * C, Op.max)
             return
         need(v, "v_d%d" % (k - 1))
-        if k == 5:
-            inc(v.tensor_tensor(T.d[:, :], zb[5][:, 0:48], T.d4m[:, :], Op.max), "d_5")
-            return
-        inc(v.tensor_tensor(T["t%d" % k][:, :], zb[k][:, 0:48], T["d%dm" % (k - 1)][:, :], Op.max), "v_t%d" % k)
-        need(v, "v_t%d" % k)
-        ts("v_d%d" % k, T["d%dm" % k][:, :], T["t%d" % k][:, :], -C, Op.add)
+        inc(v.tensor_tensor(T.pb3[0:48, 0:128] if k == 5 else d, z, T["d%dm" % (k - 1)][0:48, :], Op.max), "v_d%d" % k)
 
-    def ids(*ks):
-        for k in ks:
-            a = T["a%d" % k]
-            need(pe, "a_id%d" % k)
-            if k == 1:
-                need(pe, "c_wg")
-            for b in range(6):
-                if k == 5 and b == 3:
-                    need(pe, "a_id6")
-                inc(pe.matmul(zb[k][:, b:48:6], a[:, 128 * b:128 * b + 128], T.wg[:, :], True, True), "p_z%d" % k)
-
-    for k in range(1, 6):
-        lst, a = T["list%d" % k], T["a%d" % k]
-        if k == 1:
-            need(v, "l_l", "r_own", "r_arr", "e_halo", "e_main")
-            inc(v.tensor_tensor(T.m1[:, :], T.r[:, 0:32].indirect(T.letl[:, 0:48]), T.e[:, 1:1 + S], Op.mult), "v_m1")
-            need(pe, "b_base")
-            wrap(T.m1, 48, "p_list2", True, "v_m1")
-            need(act, "w2_in", "r_all", "l_cc")
-            inc(act.activation(T.rid[:, :], win2.indirect(T.rall[:, 0:1]), Act.Copy), "a_rid")
-            need(act, "a_rid")
-            inc(act.activation(a[:, :], T.rid[:, 0:16].indirect(T.letc[:, 0:48]), Act.Copy), "a_id1")
-            ts("c_w", T.wz[:, :], T.cf[:, :], 0.0, Op.is_equal, 256.0, Op.mult)
-            ts("c_w", T.wy[:, :], T.cf[:, :], 1.0, Op.is_equal)
-            ts("c_idf", T.idf[:, :], T.rowi[:, :], T.pf[:, :], Op.is_equal)
-            need(v, "c_w")
-            inc(v.tensor_tensor(T.wc[:, :], T.wz[:, :], T.wy[:, :], Op.add), "c_wc")
-            need(v, "c_wc")
-            ts("c_wg", T.wg[:, :], T.grp[:, :], T.wc[:, :], Op.mult)
-            continue
-        need(v, "p_list%d" % k)
-        inc(v.tensor_copy(lst[:, :], T.pb4[:, 48 * (k - 1):48 * k]), "v_list%d" % k)
-        need(v, "v_list%d" % k)
-        need(act, "v_list%d" % k)
-        if k == 2:
-            need(v, "w_arr")
-        if k < 5:
-            mk = T["m%d" % k]
-            inc(v.tensor_tensor(mk[:, :], win.indirect(lst[:, 0:48]), T.e[:, k:k + S], Op.mult), "v_m%d" % k)
-            inc(act.activation(a[:, :], win2.indirect(lst[:, 0:48]), Act.Copy), "a_id%d" % k)
-            need(pe, "v_list%d" % k)
-            wrap(mk, 48 * k, "p_list%d" % (k + 1), True, "v_m%d" % k)
-            if k == 2:
-                ids(1)
-            if k == 3:
-                ids(2, 3)
-                keep(1)
-            if k == 4:
-                keep(2)
-                keep(3)
-                ids(4)
-        else:
-            need(v, "w2_in")
-            inc(v.tensor_copy(a[:, 0:384], win2.indirect(lst[:, 0:24])), "a_id5")
-            inc(act.activation(a[:, 384:768], win2.indirect(lst[:, 24:48]), Act.Copy), "a_id6")
-            ids(5)
-            keep(4)
+    need(v, "r_arr", "l_l", "e_halo", "e_main", "z_rl")
+    step(2, "a")
+    for q in range(n):
+        ts("r_l", T.rl[:, 5 * q:5 * q + 4], T.r[:, R * q + 64 + 4 * q:R * q + 68 + 4 * q], 256.0 + M * q, Op.add)
+    step(2, "b")
+    need(act, "w2_in", "r_all")
+    inc(act.activation(T.rid[:, :], win2.indirect(T.rall[:, 0:1]), Act.Copy), "a_rid")
+    need(act, "a_rid", "l_cc")
+    inc(act.activation(T.a1[:, :], T.rid[:, 0:16].indirect(T.letc[:, 0:48]), Act.Copy), "a_id1")
+    need(act, "r_l")
+    inc(act.activation(T.ridb[:, :], win2.indirect(T.rl[:, 0:20]), Act.Copy), "a_ridb")
+    need(act, "a_ridb", "l_l")
+    inc(act.activation(T.a2[:, :], T.ridb[:, 0:4 * R].indirect(T.letl[:, 0:48]), Act.Copy), "a_id2")
+    need(pe, "b_base")
+    wrap(2, "a")
+    wrap(2, "b")
+    need(pe, "z_ones", "c_wg")
+    ids(1)
+    take(3, "a")
+    take(3, "b")
+    need(act, "v_list3a", "v_list3b")
+    inc(act.activation(T.a3[:, :], win2.indirect(T.list3[:, 0:48]), Act.Copy), "a_id3")
+    need(v, "w_arr")
+    step(3, "a")
+    step(3, "b")
+    wrap(3, "a")
+    wrap(3, "b")
+    ids(2)
+    keep(1)
+    for f in "ab":
+        take(4, f)
+        step(4, f)
+        h = part[f]
+        need(act, "v_list4" + f)
+        inc(act.activation(T.a4[:, H * h:H * h + H], win2.indirect(T.list4[:, 24 * h:24 * h + 24]), Act.Copy), "a_id4")
+        wrap(4, f)
+        if f == "a":
+            ids(3)
+    ids(4)
+    keep(2)
+    keep(3)
+    need(v, "w2_in")
+    for f in "ab":
+        take(5, f)
+        h = part[f]
+        inc(v.tensor_copy(T.a5[:, H * h:H * h + 192], win2.indirect(T.list5[:, 24 * h:24 * h + 12])), "v_id5" + f)
+        need(act, "v_list5" + f)
+        inc(act.activation(T.a5[:, H * h + 192:H * h + H], win2.indirect(T.list5[:, 24 * h + 12:24 * h + 24]), Act.Copy),
+            "a_id5" if f == "a" else "b_id5")
+    z5 = zb[5]
+    for waits, pieces in (("v_id5a", ((0, 0, 128), (1, 0, 64))), ("a_id5", ((1, 64, 128), (2, 0, 128))),
+                          ("v_id5b", ((3, 0, 128), (4, 0, 64))), ("b_id5", ((4, 64, 128), (5, 0, 128)))):
+        need(pe, waits)
+        for b, lo, hi in pieces:
+            call = pe.matmul(z5[0:48, lo:hi], T.wg[:, 48 * b:48 * b + 48], T.a5[:, 128 * b + lo:128 * b + hi],
+                             b == 0, b == 5)
+    inc(call, "p_z5")
+    keep(4)
     keep(5)
 
-    need(pe, "d_5", "c_idf")
-    inc(pe.transpose(T.pb3[0:48, 0:128], T.d[:, :], T.idf[:, :]), "p_t")
-    need(v, "p_t")
-    ts("rr_ok", T.rr[0:48, :], T.pb3[0:48, 0:128], BIG, Op.add, -BIG, Op.add)
+    d = T.pb3[0:48, 0:128]
+    need(v, "v_d5")
+    ts("rr_ok", T.rr[0:48, :], d, BIG, Op.add, -BIG, Op.add)
     need(v, "rr_ok")
-    inc(v.tensor_tensor(T.yi[0:48, :], T.pb3[0:48, 0:128], T.rr[0:48, :], Op.subtract), "yi_ok")
+    inc(v.tensor_tensor(T.yi[0:48, :], d, T.rr[0:48, :], Op.subtract), "yi_ok")
     need(act, "rr_ok")
     inc(act.activation(T.yl[0:48, :], T.rr[0:48, :], Act.Copy, bias=5.0, scale=1.0 / C), "yl_ok")
     need(act, "yl_ok")
@@ -306,4 +344,4 @@ def rank_program(g, core, T, topo):
     inc(sp.dma_start(T.yid[:, :], T.yi[0:48, :]), "st_id", 16)
     need(act, "st_len")
     need(sp, "st_id")
-    need(g, "sm_out", "w_out", "r_out")
+    need(g, "sm_out", "id_out", "w_out", "r_out")

@@ -3,34 +3,36 @@ from concourse.mybir import AluOpType as Op, ActivationFunctionType as Act, Axis
 
 S, M = 768, 512
 H = S // 2
-MW = 16
+MW = 80
 R = 80
 C = 131072.0
 BIG = 1.5 * 2.0 ** 40
-SCRATCH = {"x": ("sbuf", [128, 4, 8, 16], "int32"), "xb": ("sbuf", [128, 8, 4, 16], "bfloat16"),
-           "ido": ("dram", [128, 64], "bfloat16"), "idr": ("dram", [4, 128, 64], "bfloat16")}
-for _t, _s in (("int32", "li192 ti64 thi64 tlo64 rw1 pi1 ci1 oi1 rowi128 rowq128 ln48 lq48"),
-               ("float32", "tz64 pf1 gf1 cf1 ncf1 ncg1 wz1 wx1 wy1 wc1 basec1 rootc1 grp8 rr128 yl128 yi128"),
-               ("uint16", "rown2 rall2 lown4 rl20 letl48 letc48"),
-               ("bfloat16", "l192 hi64 lo64 sm64 w2048 v2048 ab768 e784 bm784 sel2048 ones128 neg48 gbs512 idb128 wg288 baseb48 "
-                            "sb48 r320 rid16 ridb320")):
+NONE = -2.0 ** 24
+SCRATCH = {"x": ("sbuf", [128, 4, 8, 16], "int32"), "xb": ("sbuf", [128, 8, 4, 16], "bfloat16")}
+for _t, _s in (("int32", "li52 lh4 ti64 thi64 tlo64 rw1 pi1 ci1 gi1 oi1 lq48 lp48 ln48 lm48 ls48 rowi128 yv64"),
+               ("float32", "tz64 pf1 gf1 cf1 hf1 basec1 rootc1 grp8 best192 rr192 yl192 yi192"),
+               ("uint16", "rown2 rall2 lown4 rl20 letl48 lx52"),
+               ("bfloat16", "sm320 lf4 w2048 v2048 e832 sel2048 y1024 ones192 far32 idb128 sha128 shb128 u16 base48 "
+                            "r320 rid16 ridb320")):
     for _n in _s.split():
         _b = _n.rstrip("0123456789")
         SCRATCH[_b] = ("sbuf", [128, int(_n[len(_b):])], _t)
-for _k in range(1, 6):
+for _k in (3, 4, 5):
     SCRATCH["list%d" % _k] = ("sbuf", [128, 48], "uint16")
+for _k in range(1, 6):
     SCRATCH["a%d" % _k] = ("sbuf", [128, S], "bfloat16")
+for _k in (2, 3, 4):
     SCRATCH["m%d" % _k] = ("sbuf", [128, S], "bfloat16")
-    SCRATCH["d%dm" % _k] = ("sbuf", [128, 128], "float32")
 for _k in range(8):
     SCRATCH["pb%d" % _k] = ("psum", [128, 512], "float32")
-SEMAPHORES = ("ld_lett ld_tid ld_root ld_kid sm_arr w_arr r_arr sm_out w_out r_out w2_in st_id st_len iota z_w2 z_w3 z_sel z_sel2 "
-              "z_ones z_sm z_rl c_a c_b c_gs c_id c_grp c_bc c_w c_wx c_wc c_wg c_sel s_th s_id s_sm id_st id_arr id_out s_l "
-              "p_l0 p_l1 o_ls o_l2 w_own r_tmp r_own e_abs e_main b_mul b_h p_halo e_halo r_col r_all p_c1 p_c2 l_n l_cc l_q l_s "
-              "b_base l_l r_l a_rid a_ridb rr_ok yi_ok yl_ok x_conv0 x_conv1 p_x0 p_x1 p_x2 p_x3 v_id5a v_id5b c_gf z_wg").split()
-for _k in range(1, 6):
-    SEMAPHORES += [_n % _k for _n in ("p_z%d", "v_d%d", "a_id%d", "b_id%d", "v_m%da", "v_m%db", "p_list%da", "p_list%db",
-                                      "v_list%da", "v_list%db")]
+SEMAPHORES = ("ld_lett ld_halo ld_tid ld_tid2 ld_root ld_kid0 ld_kid1 ld_kid2 ld_kid3 sm_arr w_arr r_arr sm_out w_out r_out st_id "
+              "st_len iota iota2 z_sel z_sel2 z_y z_ones z_sm z_sh z_rl c_a c_b c_o c_bc c_id c_u c_sh c_grp c_y c_sel s_th "
+              "s_id s_sm l_x l_a l_b l_c l_e l_l l_e2 l_l2 b_base p_halo l_h l_hx o_ls o_l2 w_own r_tmp r_own e_main e_halo r_col "
+              "r_all r_l a_rid a_ridb a_id1 a_id2 a_id3 x_conv0 x_conv1 p_x0 p_x1 p_x2 p_x3 p_v0 p_v1 p_v2 p_v3 v_in v_in2 "
+              "p_z1 p_z2 p_z3 p_z4 d1 d2 d3 d4 a_id5").split()
+for _f in "ab":
+    SEMAPHORES += [_n + _f for _n in ("v_m2", "v_m3", "v_m4", "p_list3", "p_list4", "p_list5", "v_list3", "v_list4", "v_list5",
+                                      "a_id4", "v_id5", "p_z5", "d5", "rr_ok", "yi_ok", "yl_ok")]
 
 
 def rank_program(g, core, T, topo):
@@ -72,79 +74,65 @@ def rank_program(g, core, T, topo):
         g.remote_dma_fused(tr, local_sem=T.sem[out])
 
     c0, cw, r0, o = MW * rank, M * rank, R * rank, 4 * rank
+    lo64, hi64 = slice(0, 64), slice(64, 128)
     inc(act.dma_start(T.rw[:, 0:1], T.kid[:, 16:32]), "ld_root", 16)
-    inc(sp.dma_start(T.li[0:32, :], T.lett[:, :]), "ld_lett", 16)
-    inc(sp.dma_start(T.ti[0:64, :], T.tid[:, :]), "ld_tid", 16)
+    inc(sp.dma_start(T.ti[lo64, :], T.tid[:, :]), "ld_tid", 16)
+    inc(sp.dma_start(T.lh[0:8, :], T.lett[:, 0:4]), "ld_halo", 16)
+    inc(act.dma_start(T.ti[hi64, :], T.tid[:, :]), "ld_tid2", 16)
     for q4 in range(4):
-        inc((sp, act)[q4 % 2].dma_start(T.x[:, q4, :, :], T.kid[q4:8:4, :]), "ld_kid", 16)
+        inc((act, sp)[q4 % 2].dma_start(T.x[:, q4, :, :], T.kid[q4:8:4, :]), "ld_kid%d" % q4, 16)
+    inc(sp.dma_start(T.li[:, 0:48], T.lett[:, :]), "ld_lett", 16)
 
     inc(g.iota(T.pi[:, :], [[0, 1]], 0, 1), "iota")
     inc(g.iota(T.rowi[:, :], [[1, 128]], 0, 0), "iota")
-    inc(g.iota(T.v[:, 1024:2048], [[0, 1024]], 0, 0, allow_small_or_imprecise_dtypes=True), "z_w3")
+    inc(g.iota(T.yv[:, :], [[1, 8], [8, 8]], 0, 0), "iota2")
+    inc(v.memset(T.sm[:, c0:c0 + 16], 0.0), "z_sm")
     inc(v.memset(T.sel[:, 0:1024], 0.0), "z_sel")
-    inc(v.memset(T.sm[:, c0:c0 + MW], 0.0), "z_sm")
-    inc(v.memset(T.ones[:, :], 1.0), "z_ones")
-    inc(v.memset(T.neg[:, :], -C), "z_ones")
     need(v, "iota")
     ts("c_a", T.ci[:, :], T.pi[:, :], 15, Op.bitwise_and)
-    ts("c_a", T.rowq[:, :], T.rowi[:, :], 2, Op.arith_shift_right, 28, Op.bitwise_and)
+    ts("c_a", T.gi[:, :], T.pi[:, :], 4, Op.arith_shift_right)
     inc(v.tensor_copy(T.pf[:, :], T.pi[:, :]), "c_a")
+    inc(v.memset(T.ones[:, :], 1.0), "z_ones")
+    inc(v.memset(T.far[:, :], C), "z_ones")
     need(v, "c_a")
-    ts("c_b", T.ncf[:, :], T.ci[:, :], -1.0, Op.mult)
-    inc(v.tensor_copy(T.cf[:, :], T.ci[:, :]), "c_b")
-    for s in range(4):
-        ts("c_gs", T.gbs[0:32, 128 * s:128 * s + 128], T.rowq[0:32, :], float(s), Op.add, T.pf[0:32, :], Op.is_equal)
     ts("c_id", T.idb[:, :], T.rowi[:, :], T.pf[:, :], Op.is_equal)
+    inc(v.tensor_copy(T.cf[:, :], T.ci[:, :]), "c_b")
+    inc(v.tensor_copy(T.gf[:, :], T.gi[:, :]), "c_b")
+    ts("c_b", T.hf[:, :], T.pf[:, :], 16.0, Op.mult, 15.0, Op.add)
+    ts("c_o", T.oi[:, :], T.ci[:, :], 2, Op.arith_shift_right)
     need(act, "z_sel")
+    inc(act.activation(T.y[:, :], T.sel[:, 0:1024], Act.Copy), "z_y")
     inc(act.activation(T.sel[:, 1024:2048], T.sel[:, 0:1024], Act.Copy), "z_sel2")
-    inc(act.activation(T.v[:, 0:1024], T.sel[:, 0:1024], Act.Copy), "z_w2")
-    inc(act.activation(T.wg[:, :], T.sel[:, 0:288], Act.Copy), "z_wg")
-    need(act, "c_a", "c_b")
-    inc(act.activation(T.ncg[:, :], T.ncf[:, :], Act.Copy, scale=0.0625), "c_bc")
-    inc(act.activation(T.wz[:, :], T.cf[:, :], Act.Relu, bias=1.0, scale=-1.0), "c_w")
-    inc(act.activation(T.wx[:, :], T.cf[:, :], Act.Abs, bias=T.neg1[:, :]) if False else
-        act.activation(T.wx[:, :], T.cf[:, :], Act.Square, bias=-1.0), "c_wx")
-    need(act, "c_bc")
-    inc(act.activation(T.gf[:, :], T.pf[:, :], Act.Identity, bias=T.ncg[:, :], scale=0.0625), "c_gf")
-    need(act, "c_wx")
-    inc(act.activation(T.wy[:, :], T.wx[:, :], Act.Relu, bias=1.0, scale=-1.0), "c_w")
-    need(act, "c_w")
-    inc(act.activation(T.wc[:, :], T.wz[:, :], Act.Identity, bias=T.wy[:, :], scale=256.0), "c_wc")
 
-    need(v, "ld_lett", "z_sm")
-    inc(v.tensor_copy(T.l[0:32, :], T.li[0:32, :]), "s_l")
     need(v, "ld_tid")
-    i64 = slice(0, 64)
-    ts("s_th", T.thi[i64, :], T.ti[i64, :], 8, Op.arith_shift_right)
-    ts("s_th", T.tlo[i64, :], T.ti[i64, :], 255, Op.bitwise_and)
-    ts("s_th", T.tz[i64, :], T.ti[i64, :], 0.0, Op.is_equal, -65536.0, Op.mult)
-    inc(v.tensor_copy(T.sm[0:32, c0 + 8:c0 + 12], T.li[0:32, 0:4]), "s_sm")
-    need(v, "ld_root", "s_th")
-    inc(v.tensor_tensor(T.hi[i64, :], T.thi[i64, :], T.tz[i64, :], Op.add), "s_id")
-    inc(v.tensor_copy(T.lo[i64, :], T.tlo[i64, :]), "s_id")
+    ts("s_th", T.thi[lo64, :], T.ti[lo64, :], 65280, Op.bitwise_and)
+    ts("s_th", T.tz[lo64, :], T.ti[lo64, :], 0.0, Op.is_equal, NONE, Op.mult)
+    need(v, "ld_tid2")
+    ts("s_th", T.tlo[hi64, :], T.ti[hi64, :], 255, Op.bitwise_and)
+    need(v, "ld_root", "z_sm")
     ts("s_sm", T.sm[:, c0:c0 + 1], T.rw[:, 0:1], -256.0, Op.add)
-    inc(v.tensor_copy(T.rown[:, 0:1], T.rw[:, 0:1]), "o_ls")
-    need(g, "s_sm")
+    need(v, "s_th")
+    inc(v.tensor_tensor(T.sm[lo64, c0 + 16:c0 + 80], T.thi[lo64, :], T.tz[lo64, :], Op.add), "s_id")
+    inc(v.tensor_copy(T.sm[hi64, c0 + 16:c0 + 80], T.tlo[hi64, :]), "s_id")
+    need(v, "ld_halo")
+    inc(v.tensor_copy(T.sm[0:8, c0 + 8:c0 + 12], T.lh[0:8, :]), "s_sm")
+    need(g, "s_sm", "s_id")
     spread(T.sm[:, c0:c0 + MW], T.sm[:, c0:c0 + MW], "sm_arr", "sm_out")
-    need(sp, "s_id")
-    inc(sp.dma_start(T.ido[0:64, :], T.hi[i64, :]), "id_st", 16)
-    inc(sp.dma_start(T.ido[64:128, :], T.lo[i64, :]), "id_st", 16)
-    need(g, "id_st")
-    spread(T.ido[:, :], T.idr[rank], "id_arr", "id_out")
-    need(pe, "s_l", "c_gs")
-    for s in range(4):
-        inc(pe.matmul(T["pb%d" % (s // 2)][:, 192 * (s % 2):192 * (s % 2) + 192], T.gbs[0:32, 128 * s:128 * s + 128],
-                      T.l[0:32, :], True, True), "p_l%d" % (s // 2))
-    for j in range(2):
-        need(act, "p_l%d" % j)
-        inc(act.activation(T.ab[:, H * j:H * j + H], T["pb%d" % j][:, 0:H], Act.Abs, bias=T.ncf[:, :]), "e_abs")
+    inc(v.tensor_copy(T.rown[:, 0:1], T.rw[:, 0:1]), "o_ls")
+    need(v, "c_b", "c_o")
+    ts("c_u", T.u[:, :], T.rowi[:, 0:16], T.cf[:, :], Op.is_equal)
+    ts("c_grp", T.grp[:, :], T.rowi[:, 0:8], T.gf[:, :], Op.is_equal)
+    ts("c_sh", T.shb[:, :], T.rowi[:, :], T.hf[:, :], Op.is_equal)
+    need(v, "iota2", "z_y", "c_id")
+    ts("c_y", T.y[:, 0:1024:16], T.yv[:, :], T.pf[:, :], Op.is_equal)
+    ts("c_y", T.y[:, 1:1024:16], T.yv[:, :], 64.0, Op.add, T.pf[:, :], Op.is_equal)
 
-    need(v, "ld_kid")
-    for par in range(2):
-        for q4 in range(4):
+    for q4 in range(4):
+        need(v, "ld_kid%d" % q4)
+        for par in range(2):
             ts("x_conv%d" % par, T.xb[:, par:8:2, q4, :], T.x[:, q4, par:8:2, :], -256.0, Op.add)
-    need(pe, "c_id")
     xbank = [T.pb2, T.pb3, T.pb4, T.pb6]
+    need(pe, "c_id")
     for u in (0, 2, 1, 3):
         need(pe, "x_conv%d" % (u % 2))
         for j in range(2):
@@ -167,81 +155,80 @@ def rank_program(g, core, T, topo):
     need(g, "w_own")
     spread(T.w[:, cw:cw + M], T.w[:, cw:cw + M], "w_arr", "w_out")
 
-    need(v, "c_gf")
-    ts("c_grp", T.grp[:, :], T.rowi[:, 0:8], T.gf[:, :], Op.is_equal)
-    need(v, "c_grp", "z_sel", "z_sel2", "z_w2", "z_wg", "z_ones")
+    need(v, "ld_lett")
+    inc(v.tensor_copy(T.lx[:, 0:48], T.li[:, 0:48]), "l_x")
+    need(act, "l_x", "c_u")
+    inc(act.activation(T.e[:, 32:S], T.u[:, 0:16].indirect(T.lx[:, 2:48]), Act.Copy), "e_main")
+    ts("l_a", T.lq[:, :], T.li[:, 0:48], 12, Op.bitwise_and)
+    ts("l_a", T.ln[:, :], T.li[:, 0:48], 16.0, Op.mult)
+    inc(v.tensor_copy(T.sha[:, 0:127], T.idb[:, 1:128]), "z_sh")
+    need(v, "l_a")
+    ts("l_b", T.lp[:, :], T.lq[:, :], 4.0, Op.mult)
+    ts("b_base", T.base[:, :], T.lq[:, :], 128.0, Op.mult, 256.0, Op.add)
+    need(v, "z_sh")
+    inc(v.memset(T.sha[:, 15:128:16], 0.0), "c_sh")
+    need(v, "l_b")
+    inc(v.tensor_tensor(T.lm[:, :], T.ln[:, :], T.lp[:, :], Op.add), "l_c")
+    inc(v.tensor_copy(T.lf[:, :], T.li[:, 0:4]), "l_h")
+    need(v, "l_c")
+    inc(v.tensor_tensor(T.ls[:, 0:24], T.lm[:, 0:24], T.li[:, 1:25], Op.add), "l_e")
+    inc(v.memset(T.rl[:, :], 0), "z_rl")
+    need(v, "l_e")
+    inc(v.tensor_copy(T.letl[:, 0:24], T.ls[:, 0:24]), "l_l")
+    need(v, "c_grp", "z_sel", "z_sel2", "z_ones")
     for h in range(8):
         ts("c_sel", T.sel[:, 16 * h:2048:129], T.ones[:, 0:16], T.grp[:, h:h + 1], Op.mult)
-
-    need(act, "e_abs")
-    inc(act.activation(T.e[:, 0:S], T.ab[:, :], Act.Relu, bias=1.0, scale=-1.0), "e_main")
-    need(act, "e_main")
-    inc(act.activation(T.bm[:, 0:S], T.e[:, 0:S], Act.Copy, scale=T.cf[:, :]), "b_mul")
-    need(act, "c_wc", "z_wg", "c_grp")
-    for b in range(6):
-        inc(act.activation(T.wg[:, 48 * b + b:48 * b + 48:6], T.grp[:, :], Act.Copy, scale=T.wc[:, :]), "c_wg")
+    ts("c_bc", T.basec[:, :], T.oi[:, :], 512.0, Op.mult, 1024.0, Op.add)
 
     cn = MW * ((rank + 1) % n)
-    need(pe, "s_sm", "sm_arr")
-    inc(pe.matmul(T.pb5[:, 0:4], T.gbs[0:32, 0:128], T.sm[0:32, cn + 8:cn + 12], True, True), "p_halo")
-    need(v, "p_halo", "c_b")
-    ts("b_h", T.bm[:, S:S + 1], T.pb5[:, 0:1], T.cf[:, :], Op.is_equal, T.cf[:, :], Op.mult)
-    ts("e_halo", T.e[:, S:S + 4], T.pb5[:, 0:4], T.cf[:, :], Op.is_equal)
-
-    need(pe, "c_sel", "b_mul")
-    for i in range(16):
-        call = pe.matmul(T.pb6[:, 0:48], T.sel[:, 128 * i:128 * i + 128], T.bm[:, i:i + 753:16], i == 0, i == 15)
-    inc(call, "p_c1")
-    for i in range(16):
-        if i == 15:
-            need(pe, "b_h")
-        pe.matmul(T.pb7[:, 0:48], T.sel[:, 128 * i:128 * i + 128], T.bm[:, i + 1:i + 754:16], i == 0, False)
-    need(v, "p_c1")
-    ts("l_n", T.ln[:, :], T.pb6[:, 0:48], 16.0, Op.mult)
-    need(v, "l_n")
-    ts("l_q", T.lq[:, :], T.ln[:, :], 2, Op.arith_shift_right, 48, Op.bitwise_and)
-    inc(v.tensor_copy(T.letc[:, :], T.pb6[:, 0:48]), "l_cc")
-    need(v, "l_q")
-    inc(v.tensor_tensor(T.sb[:, :], T.ln[:, :], T.lq[:, :], Op.add), "l_s")
-    ts("b_base", T.baseb[:, :], T.lq[:, :], 32.0, Op.mult, 256.0, Op.add)
-    need(pe, "l_s")
-    inc(pe.matmul(T.pb7[:, 0:48], T.idb[:, :], T.sb[:, :], False, True), "p_c2")
-    need(v, "p_c2")
-    inc(v.tensor_copy(T.letl[:, :], T.pb7[:, 0:48]), "l_l")
-    ts("c_a", T.oi[:, :], T.ci[:, :], 2, Op.arith_shift_right)
-    inc(v.memset(T.rl[:, :], 0), "z_rl")
-    need(v, "sm_arr", "s_sm")
-    inc(v.tensor_reduce(T.rootc[:, :], T.sm[:, 0:MW * n:MW], AxisListType.X, Op.add), "r_col")
-    need(v, "c_a")
-    ts("r_col", T.basec[:, :], T.oi[:, :], 512.0, Op.mult, 1024.0, Op.add)
-    need(v, "r_col")
-    ts("r_all", T.rall[:, 0:1], T.rootc[:, :], T.basec[:, :], Op.add)
-
+    vb = [T.pb0, T.pb1, T.pb5, T.pb7]
+    need(pe, "c_y", "s_id")
     for j in range(n):
         q = (rank + j) % n
-        for queue, row, half in ((sp, 0, slice(0, 64)), (act, 1, slice(64, 128))):
-            need(queue, "id_arr" if j else "id_st")
-            if j == 0:
-                need(queue, "z_w2", "z_w3")
-            inc(queue.dma_start(T.v[row:128:16, M * q:M * q + M], T.idr[q, half, :] if j else T.ido[half, :]), "w2_in", 16)
+        if j == 1:
+            need(pe, "c_sh", "l_h", "w_own", "s_sm", "sm_arr")
+            pe.matmul(T.pb2[:, 0:4], T.sha[:, :], T.lf[:, :], True, False)
+            inc(pe.matmul(T.pb2[:, 0:4], T.shb[0:8, :], T.sm[0:8, cn + 8:cn + 12], False, True), "p_halo")
+        for b in range(8):
+            inc(pe.matmul(vb[j][:, 64 * b:64 * b + 64], T.y[:, 128 * b:128 * b + 128], T.sm[:, MW * q + 16:MW * q + 80],
+                          True, True), "p_v%d" % j)
+        if j < n - 1:
+            need(act, "p_v%d" % j)
+            inc(act.activation(T.v[:, M * q:M * q + M], vb[j][:, :], Act.Copy), "v_in")
+    need(v, "p_halo")
+    inc(v.tensor_copy(T.li[:, 48:52], T.pb2[:, 0:4]), "l_hx")
+    inc(v.tensor_copy(T.lx[:, 48:52], T.pb2[:, 0:4]), "l_hx")
+    need(v, "sm_arr", "s_sm")
+    inc(v.tensor_reduce(T.rootc[:, :], T.sm[:, 0:MW * n:MW], AxisListType.X, Op.add), "r_col")
+    need(v, "l_hx", "c_u")
+    inc(v.tensor_tensor(T.ls[:, 24:48], T.lm[:, 24:48], T.li[:, 25:49], Op.add), "l_e2")
+    inc(v.tensor_copy(T.e[:, S:S + 64], T.u[:, 0:16].indirect(T.lx[:, 48:52])), "e_halo")
+    need(v, "l_e2")
+    inc(v.tensor_copy(T.letl[:, 24:48], T.ls[:, 24:48]), "l_l2")
+    need(v, "r_col", "c_bc")
+    ts("r_all", T.rall[:, 0:1], T.rootc[:, :], T.basec[:, :], Op.add)
+    need(v, "p_v%d" % (n - 1))
+    inc(v.tensor_copy(T.v[:, M * q:M * q + M], vb[n - 1][:, :]), "v_in2")
 
     win, win2 = T.w[:, 0:4 * M], T.v[:, 0:4 * M]
-    zb = {1: T.pb0, 2: T.pb5, 3: T.pb6, 4: T.pb7, 5: T.pb1}
-    lbank = {"a": T.pb4, "b": T.pb2}
+    lbank = {"a": T.pb2, "b": T.pb3}
+    zb = {1: T.pb0, 2: T.pb1, 3: T.pb5, 4: T.pb7}
+    z5 = {"a": T.pb4, "b": T.pb6}
     part = {"a": 0, "b": 1}
 
     def step(k, f):
         h = part[f]
         src = T.r[:, 0:4 * R].indirect(T.letl[:, 24 * h:24 * h + 24]) if k == 2 else \
             win.indirect(T["list%d" % k][:, 24 * h:24 * h + 24])
-        inc(v.tensor_tensor(T["m%d" % k][:, H * h:H * h + H], src, T.e[:, k + H * h:k + H * h + H], Op.mult), "v_m%d%s" % (k, f))
+        inc(v.tensor_tensor(T["m%d" % k][:, H * h:H * h + H], src, T.e[:, 16 * k + H * h:16 * k + H * h + H], Op.mult),
+            "v_m%d%s" % (k, f))
 
     def wrap(k, f):
         h = part[f]
         if k > 2:
             need(pe, "v_list%d%s" % (k, f))
-        out = lbank[f][:, 32 * (k - 2):32 * (k - 2) + 24]
-        pe.matmul(out, T.idb[:, :], T.baseb[:, 24 * h:24 * h + 24], True, False)
+        out = lbank[f][:, 0:24]
+        pe.matmul(out, T.idb[:, :], T.base[:, 24 * h:24 * h + 24], True, False)
         need(pe, "v_m%d%s" % (k, f))
         for i in range(16):
             call = pe.matmul(out, T.sel[:, 128 * i:128 * i + 128], T["m%d" % k][:, H * h + i:H * h + H:16], False, i == 15)
@@ -250,45 +237,53 @@ def rank_program(g, core, T, topo):
     def take(k, f):
         h = part[f]
         need(v, "p_list%d%s" % (k, f))
-        inc(v.tensor_copy(T["list%d" % k][:, 24 * h:24 * h + 24], lbank[f][:, 32 * (k - 3):32 * (k - 3) + 24]),
-            "v_list%d%s" % (k, f))
+        inc(v.tensor_copy(T["list%d" % k][:, 24 * h:24 * h + 24], lbank[f][:, 0:24]), "v_list%d%s" % (k, f))
         need(v, "v_list%d%s" % (k, f))
 
-    def ids(k):
-        z = zb[k][0:48, 0:128]
-        pe.matmul(z, T.neg[0:5 - k, 0:48], T.ones[0:5 - k, :], True, False)
-        need(pe, "a_id%d" % k)
-        for b in range(6):
-            call = pe.matmul(z, T.wg[:, 48 * b:48 * b + 48], T["a%d" % k][:, 128 * b:128 * b + 128], False, b == 5)
+    def add_far(k, z):
+        pe.matmul(z, T.far[0:k, :], T.ones[0:k, 0:z.shape[1]], True, False)
+
+    def sums(k, z, col, s, last):
+        for b in range(4):
+            i = 4 * b + s
+            call = pe.matmul(z[0:32, col:col + 48], T.sel[:, 128 * i + s:128 * i + 128:4], T["a%d" % k][:, i:S:16],
+                             False, last and b == 3)
+        return call
+
+    def ids(k, *waits):
+        need(pe, *waits)
+        for s in range(4):
+            call = sums(k, zb[k], 48 * s, s, s == 3)
         inc(call, "p_z%d" % k)
 
     def keep(k):
-        need(v, "p_z%d" % k)
-        z, d = zb[k][0:48, 0:128], T["d%dm" % k][0:48, :]
-        if k == 1:
-            ts("v_d1", d, z, -5.0 * C, Op.max)
-            return
-        need(v, "v_d%d" % (k - 1))
-        inc(v.tensor_tensor(T.pb3[0:48, 0:128] if k == 5 else d, z, T["d%dm" % (k - 1)][0:48, :], Op.max), "v_d%d" % k)
+        need(v, "p_z%d" % k, "d%d" % (k - 1))
+        inc(v.tensor_tensor(T.best[0:32, :], zb[k][0:32, 0:192], T.best[0:32, :], Op.max), "d%d" % k)
 
-    need(v, "r_arr", "l_l", "e_halo", "e_main", "z_rl")
+    need(act, "v_in", "v_in2", "r_all")
+    inc(act.activation(T.rid[:, :], win2.indirect(T.rall[:, 0:1]), Act.Copy), "a_rid")
+    need(act, "a_rid")
+    inc(act.activation(T.a1[:, :], T.rid[:, 0:16].indirect(T.lx[:, 0:48]), Act.Copy), "a_id1")
+    need(v, "r_arr", "l_l", "e_main")
     step(2, "a")
+    need(v, "l_l2", "e_halo")
+    step(2, "b")
+    need(v, "z_rl")
     for q in range(n):
         ts("r_l", T.rl[:, 5 * q:5 * q + 4], T.r[:, R * q + 64 + 4 * q:R * q + 68 + 4 * q], 256.0 + M * q, Op.add)
-    step(2, "b")
-    need(act, "w2_in", "r_all")
-    inc(act.activation(T.rid[:, :], win2.indirect(T.rall[:, 0:1]), Act.Copy), "a_rid")
-    need(act, "a_rid", "l_cc")
-    inc(act.activation(T.a1[:, :], T.rid[:, 0:16].indirect(T.letc[:, 0:48]), Act.Copy), "a_id1")
     need(act, "r_l")
     inc(act.activation(T.ridb[:, :], win2.indirect(T.rl[:, 0:20]), Act.Copy), "a_ridb")
-    need(act, "a_ridb", "l_l")
+    need(act, "a_ridb", "l_l", "l_l2")
     inc(act.activation(T.a2[:, :], T.ridb[:, 0:4 * R].indirect(T.letl[:, 0:48]), Act.Copy), "a_id2")
-    need(pe, "b_base")
+    need(pe, "b_base", "c_sel", "l_hx", "z_ones")
+    for f in "ab":
+        add_far(5, z5[f][0:32, 0:96])
     wrap(2, "a")
     wrap(2, "b")
-    need(pe, "z_ones", "c_wg")
-    ids(1)
+    need(pe, "v_in", "v_in2")
+    for k in (1, 2, 3, 4):
+        add_far(k, zb[k][0:32, 0:192])
+    ids(1, "a_id1")
     take(3, "a")
     take(3, "b")
     need(act, "v_list3a", "v_list3b")
@@ -298,50 +293,49 @@ def rank_program(g, core, T, topo):
     step(3, "b")
     wrap(3, "a")
     wrap(3, "b")
-    ids(2)
-    keep(1)
+    ids(2, "a_id2")
     for f in "ab":
         take(4, f)
         step(4, f)
         h = part[f]
         need(act, "v_list4" + f)
-        inc(act.activation(T.a4[:, H * h:H * h + H], win2.indirect(T.list4[:, 24 * h:24 * h + 24]), Act.Copy), "a_id4")
+        inc(act.activation(T.a4[:, H * h:H * h + H], win2.indirect(T.list4[:, 24 * h:24 * h + 24]), Act.Copy), "a_id4" + f)
         wrap(4, f)
-        if f == "a":
-            ids(3)
-    ids(4)
-    keep(2)
-    keep(3)
-    need(v, "w2_in")
+    ids(3, "a_id3")
+    ids(4, "a_id4a", "a_id4b")
+    need(act, "p_z1")
+    inc(act.activation(T.best[0:32, :], zb[1][0:32, 0:192], Act.Relu), "d1")
+    need(v, "v_in", "v_in2")
+    take(5, "a")
+    inc(v.tensor_copy(T.a5[:, 0:H], win2.indirect(T.list5[:, 0:24])), "v_id5a")
+    take(5, "b")
+    inc(v.tensor_copy(T.a5[:, H:H + 192], win2.indirect(T.list5[:, 24:36])), "v_id5b")
+    need(act, "v_list5b")
+    inc(act.activation(T.a5[:, H + 192:S], win2.indirect(T.list5[:, 36:48]), Act.Copy), "a_id5")
+    for k in (2, 3, 4):
+        keep(k)
+    need(pe, "v_id5a", "v_id5b", "a_id5")
     for f in "ab":
-        take(5, f)
-        h = part[f]
-        inc(v.tensor_copy(T.a5[:, H * h:H * h + 192], win2.indirect(T.list5[:, 24 * h:24 * h + 12])), "v_id5" + f)
-        need(act, "v_list5" + f)
-        inc(act.activation(T.a5[:, H * h + 192:H * h + H], win2.indirect(T.list5[:, 24 * h + 12:24 * h + 24]), Act.Copy),
-            "a_id5" if f == "a" else "b_id5")
-    z5 = zb[5]
-    for waits, pieces in (("v_id5a", ((0, 0, 128), (1, 0, 64))), ("a_id5", ((1, 64, 128), (2, 0, 128))),
-                          ("v_id5b", ((3, 0, 128), (4, 0, 64))), ("b_id5", ((4, 64, 128), (5, 0, 128)))):
-        need(pe, waits)
-        for b, lo, hi in pieces:
-            call = pe.matmul(z5[0:48, lo:hi], T.wg[:, 48 * b:48 * b + 48], T.a5[:, 128 * b + lo:128 * b + hi],
-                             b == 0, b == 5)
-    inc(call, "p_z5")
-    keep(4)
-    keep(5)
+        for j in range(2):
+            call = sums(5, z5[f], 48 * j, 2 * part[f] + j, j == 1)
+        inc(call, "p_z5" + f)
 
-    d = T.pb3[0:48, 0:128]
-    need(v, "v_d5")
-    ts("rr_ok", T.rr[0:48, :], d, BIG, Op.add, -BIG, Op.add)
-    need(v, "rr_ok")
-    inc(v.tensor_tensor(T.yi[0:48, :], d, T.rr[0:48, :], Op.subtract), "yi_ok")
-    need(act, "rr_ok")
-    inc(act.activation(T.yl[0:48, :], T.rr[0:48, :], Act.Copy, bias=5.0, scale=1.0 / C), "yl_ok")
-    need(act, "yl_ok")
-    inc(act.dma_start(T.ylen[:, :], T.yl[0:48, :]), "st_len", 16)
-    need(sp, "yi_ok")
-    inc(sp.dma_start(T.yid[:, :], T.yi[0:48, :]), "st_id", 16)
+    half = {f: slice(96 * part[f], 96 * part[f] + 96) for f in "ab"}
+    for f in "ab":
+        need(v, "p_z5" + f, "d4")
+        inc(v.tensor_tensor(T.pb2[0:32, half[f]], z5[f][0:32, 0:96], T.best[0:32, half[f]], Op.max), "d5" + f)
+    for f in "ab":
+        need(v, "d5" + f)
+        ts("rr_ok" + f, T.rr[0:32, half[f]], T.pb2[0:32, half[f]], BIG, Op.add, -BIG, Op.add)
+    for f in "ab":
+        need(v, "rr_ok" + f)
+        inc(v.tensor_tensor(T.yi[0:32, half[f]], T.pb2[0:32, half[f]], T.rr[0:32, half[f]], Op.subtract), "yi_ok" + f)
+        need(act, "rr_ok" + f)
+        inc(act.activation(T.yl[0:32, half[f]], T.rr[0:32, half[f]], Act.Copy, scale=1.0 / C), "yl_ok" + f)
+    need(act, "yl_oka", "yl_okb")
+    inc(act.dma_start(T.ylen[:, :], T.yl[0:32, :]), "st_len", 16)
+    need(sp, "yi_oka", "yi_okb")
+    inc(sp.dma_start(T.yid[:, :], T.yi[0:32, :]), "st_id", 16)
     need(act, "st_len")
     need(sp, "st_id")
-    need(g, "sm_out", "id_out", "w_out", "r_out")
+    need(g, "sm_out", "w_out", "r_out")

from concourse.bass import DstId, RemoteDMATransfer
from concourse.mybir import AluOpType as Op, ActivationFunctionType as Act, AxisListType

S, M = 768, 512
H = S // 2
MW = 80
R = 80
C = 131072.0
BIG = 1.5 * 2.0 ** 40
NONE = -2.0 ** 24
SCRATCH = {"x": ("sbuf", [128, 4, 8, 16], "int32"), "xb": ("sbuf", [128, 8, 4, 16], "bfloat16")}
for _t, _s in (("int32", "li52 lh4 ti64 thi64 tlo64 rw1 pi1 ci1 gi1 oi1 lq48 lp48 ln48 lm48 ls48 rowi128 yv64"),
               ("float32", "tz64 pf1 gf1 cf1 hf1 basec1 rootc1 grp8 best192 rr192 yl192 yi192"),
               ("uint16", "rown2 rall2 lown4 rl20 letl48 lx52"),
               ("bfloat16", "sm320 lf4 w2048 v2048 e832 sel2048 y1024 ones192 far32 idb128 sha128 shb128 u16 base48 "
                            "r320 rid16 ridb320")):
    for _n in _s.split():
        _b = _n.rstrip("0123456789")
        SCRATCH[_b] = ("sbuf", [128, int(_n[len(_b):])], _t)
for _k in (3, 4, 5):
    SCRATCH["list%d" % _k] = ("sbuf", [128, 48], "uint16")
for _k in range(1, 6):
    SCRATCH["a%d" % _k] = ("sbuf", [128, S], "bfloat16")
for _k in (2, 3, 4):
    SCRATCH["m%d" % _k] = ("sbuf", [128, S], "bfloat16")
for _k in range(8):
    SCRATCH["pb%d" % _k] = ("psum", [128, 512], "float32")
SEMAPHORES = ("ld_lett ld_halo ld_tid ld_tid2 ld_root ld_kid0 ld_kid1 ld_kid2 ld_kid3 sm_arr w_arr r_arr sm_out w_out r_out st_id "
              "st_len iota iota2 z_sel z_sel2 z_y z_ones z_sm z_sh z_rl c_a c_b c_o c_bc c_id c_u c_sh c_grp c_y c_sel s_th "
              "s_id s_sm l_x l_a l_b l_c l_e l_l l_e2 l_l2 b_base p_halo l_h l_hx o_ls o_l2 w_own r_tmp r_own e_main e_halo r_col "
              "r_all r_l a_rid a_ridb a_id1 a_id2 a_id3 x_conv0 x_conv1 p_x0 p_x1 p_x2 p_x3 p_v0 p_v1 p_v2 p_v3 v_in v_in2 "
              "p_z1 p_z2 p_z3 p_z4 d1 d2 d3 d4 a_id5").split()
for _f in "ab":
    SEMAPHORES += [_n + _f for _n in ("v_m2", "v_m3", "v_m4", "p_list3", "p_list4", "p_list5", "v_list3", "v_list4", "v_list5",
                                      "a_id4", "v_id5", "p_z5", "d5", "rr_ok", "yi_ok", "yl_ok")]


def rank_program(g, core, T, topo):
    rank = T.rank_of(core)
    if rank is None:
        return
    n = len(T.cores)
    v, pe, act, sp = g.vector, g.tensor, g.scalar, g.sync
    count = {}

    def inc(call, name, by=1):
        call.then_inc(T.sem[name], by)
        count[name] = count.get(name, 0) + by

    def need(queue, *names):
        for name in names:
            queue.wait_ge(T.sem[name], count[name])

    def ts(name, out, in0, s1, op0, s2=None, op1=None):
        inc(v.tensor_scalar(out, in0, s1, None, op0) if op1 is None else v.tensor_scalar(out, in0, s1, s2, op0, op1), name)

    near = [d for d in T.cores if d != core and d in topo.cores_of(core)]
    far = [d for d in T.cores if d != core and d not in topo.cores_of(core)]
    far_e = [e for e in range(16) if all(e in topo.engines(core, d) for d in far)]
    near_e = [e for e in range(16) if all(e in topo.engines(core, d) for d in near) and e not in far_e]
    near_e = near_e[:len(far_e) * len(near) // len(far)]

    def spread(src, dst, arr, out):
        tr = []
        for ds, es in ((far, far_e), (near, near_e)):
            ids = []
            for d in ds:
                rid, pid = topo.addr(d, core)
                ids.append(DstId(rid=rid, pnc=pid))
            tr.append(RemoteDMATransfer(dst_ids=ids, dma_engine_mask=sum(1 << e for e in es),
                                        remote_sem=T.sem[arr], srcs=[src], dsts=[dst for _ in ds]))
            count[out] = count.get(out, 0) + len(es)
            count[arr] = count.get(arr, 0) + len(es) * len(ds)
        g.remote_dma_fused(tr, local_sem=T.sem[out])

    c0, cw, r0, o = MW * rank, M * rank, R * rank, 4 * rank
    lo64, hi64 = slice(0, 64), slice(64, 128)
    inc(act.dma_start(T.rw[:, 0:1], T.kid[:, 16:32]), "ld_root", 16)
    inc(sp.dma_start(T.ti[lo64, :], T.tid[:, :]), "ld_tid", 16)
    inc(sp.dma_start(T.lh[0:8, :], T.lett[:, 0:4]), "ld_halo", 16)
    inc(act.dma_start(T.ti[hi64, :], T.tid[:, :]), "ld_tid2", 16)
    for q4 in range(4):
        inc((act, sp)[q4 % 2].dma_start(T.x[:, q4, :, :], T.kid[q4:8:4, :]), "ld_kid%d" % q4, 16)
    inc(sp.dma_start(T.li[:, 0:48], T.lett[:, :]), "ld_lett", 16)

    inc(g.iota(T.pi[:, :], [[0, 1]], 0, 1), "iota")
    inc(g.iota(T.rowi[:, :], [[1, 128]], 0, 0), "iota")
    inc(g.iota(T.yv[:, :], [[1, 8], [8, 8]], 0, 0), "iota2")
    inc(v.memset(T.sm[:, c0:c0 + 16], 0.0), "z_sm")
    inc(v.memset(T.sel[:, 0:1024], 0.0), "z_sel")
    need(v, "iota")
    ts("c_a", T.ci[:, :], T.pi[:, :], 15, Op.bitwise_and)
    ts("c_a", T.gi[:, :], T.pi[:, :], 4, Op.arith_shift_right)
    inc(v.tensor_copy(T.pf[:, :], T.pi[:, :]), "c_a")
    inc(v.memset(T.ones[:, :], 1.0), "z_ones")
    inc(v.memset(T.far[:, :], C), "z_ones")
    need(v, "c_a")
    ts("c_id", T.idb[:, :], T.rowi[:, :], T.pf[:, :], Op.is_equal)
    inc(v.tensor_copy(T.cf[:, :], T.ci[:, :]), "c_b")
    inc(v.tensor_copy(T.gf[:, :], T.gi[:, :]), "c_b")
    ts("c_b", T.hf[:, :], T.pf[:, :], 16.0, Op.mult, 15.0, Op.add)
    ts("c_o", T.oi[:, :], T.ci[:, :], 2, Op.arith_shift_right)
    need(act, "z_sel")
    inc(act.activation(T.y[:, :], T.sel[:, 0:1024], Act.Copy), "z_y")
    inc(act.activation(T.sel[:, 1024:2048], T.sel[:, 0:1024], Act.Copy), "z_sel2")

    need(v, "ld_tid")
    ts("s_th", T.thi[lo64, :], T.ti[lo64, :], 65280, Op.bitwise_and)
    ts("s_th", T.tz[lo64, :], T.ti[lo64, :], 0.0, Op.is_equal, NONE, Op.mult)
    need(v, "ld_tid2")
    ts("s_th", T.tlo[hi64, :], T.ti[hi64, :], 255, Op.bitwise_and)
    need(v, "ld_root", "z_sm")
    ts("s_sm", T.sm[:, c0:c0 + 1], T.rw[:, 0:1], -256.0, Op.add)
    need(v, "s_th")
    inc(v.tensor_tensor(T.sm[lo64, c0 + 16:c0 + 80], T.thi[lo64, :], T.tz[lo64, :], Op.add), "s_id")
    inc(v.tensor_copy(T.sm[hi64, c0 + 16:c0 + 80], T.tlo[hi64, :]), "s_id")
    need(v, "ld_halo")
    inc(v.tensor_copy(T.sm[0:8, c0 + 8:c0 + 12], T.lh[0:8, :]), "s_sm")
    need(g, "s_sm", "s_id")
    spread(T.sm[:, c0:c0 + MW], T.sm[:, c0:c0 + MW], "sm_arr", "sm_out")
    inc(v.tensor_copy(T.rown[:, 0:1], T.rw[:, 0:1]), "o_ls")
    need(v, "c_b", "c_o")
    ts("c_u", T.u[:, :], T.rowi[:, 0:16], T.cf[:, :], Op.is_equal)
    ts("c_grp", T.grp[:, :], T.rowi[:, 0:8], T.gf[:, :], Op.is_equal)
    ts("c_sh", T.shb[:, :], T.rowi[:, :], T.hf[:, :], Op.is_equal)
    need(v, "iota2", "z_y", "c_id")
    ts("c_y", T.y[:, 0:1024:16], T.yv[:, :], T.pf[:, :], Op.is_equal)
    ts("c_y", T.y[:, 1:1024:16], T.yv[:, :], 64.0, Op.add, T.pf[:, :], Op.is_equal)

    for q4 in range(4):
        need(v, "ld_kid%d" % q4)
        for par in range(2):
            ts("x_conv%d" % par, T.xb[:, par:8:2, q4, :], T.x[:, q4, par:8:2, :], -256.0, Op.add)
    xbank = [T.pb2, T.pb3, T.pb4, T.pb6]
    need(pe, "c_id")
    for u in (0, 2, 1, 3):
        need(pe, "x_conv%d" % (u % 2))
        for j in range(2):
            for a in range(2):
                p = slice(64 * a, 64 * a + 64)
                inc(pe.matmul(xbank[u][p, j:128:2], T.xb[p, u + 4 * j, :, :], T.idb[p, p], True, True), "p_x%d" % u)
    for u in (0, 2, 1, 3):
        queue = (act, v)[u % 2]
        need(queue, "p_x%d" % u)
        land, bank = T.w[:, cw + u:cw + M:4], xbank[u][:, 0:128]
        inc(act.activation(land, bank, Act.Copy) if u % 2 == 0 else v.tensor_copy(land, bank), "w_own")
    need(v, "w_own", "o_ls")
    inc(v.tensor_copy(T.r[:, r0 + 64:r0 + 80], T.w[:, cw:cw + M].indirect(T.rown[:, 0:1])), "r_tmp")
    need(v, "r_tmp")
    ts("o_l2", T.lown[:, 0:4], T.r[:, r0 + 64 + o:r0 + 68 + o], 256.0, Op.add)
    need(v, "o_l2")
    inc(v.tensor_copy(T.r[:, r0:r0 + 64], T.w[:, cw:cw + M].indirect(T.lown[:, 0:4])), "r_own")
    need(g, "r_tmp", "r_own")
    spread(T.r[:, r0:r0 + R], T.r[:, r0:r0 + R], "r_arr", "r_out")
    need(g, "w_own")
    spread(T.w[:, cw:cw + M], T.w[:, cw:cw + M], "w_arr", "w_out")

    need(v, "ld_lett")
    inc(v.tensor_copy(T.lx[:, 0:48], T.li[:, 0:48]), "l_x")
    need(act, "l_x", "c_u")
    inc(act.activation(T.e[:, 32:S], T.u[:, 0:16].indirect(T.lx[:, 2:48]), Act.Copy), "e_main")
    ts("l_a", T.lq[:, :], T.li[:, 0:48], 12, Op.bitwise_and)
    ts("l_a", T.ln[:, :], T.li[:, 0:48], 16.0, Op.mult)
    inc(v.tensor_copy(T.sha[:, 0:127], T.idb[:, 1:128]), "z_sh")
    need(v, "l_a")
    ts("l_b", T.lp[:, :], T.lq[:, :], 4.0, Op.mult)
    ts("b_base", T.base[:, :], T.lq[:, :], 128.0, Op.mult, 256.0, Op.add)
    need(v, "z_sh")
    inc(v.memset(T.sha[:, 15:128:16], 0.0), "c_sh")
    need(v, "l_b")
    inc(v.tensor_tensor(T.lm[:, :], T.ln[:, :], T.lp[:, :], Op.add), "l_c")
    inc(v.tensor_copy(T.lf[:, :], T.li[:, 0:4]), "l_h")
    need(v, "l_c")
    inc(v.tensor_tensor(T.ls[:, 0:24], T.lm[:, 0:24], T.li[:, 1:25], Op.add), "l_e")
    inc(v.memset(T.rl[:, :], 0), "z_rl")
    need(v, "l_e")
    inc(v.tensor_copy(T.letl[:, 0:24], T.ls[:, 0:24]), "l_l")
    need(v, "c_grp", "z_sel", "z_sel2", "z_ones")
    for h in range(8):
        ts("c_sel", T.sel[:, 16 * h:2048:129], T.ones[:, 0:16], T.grp[:, h:h + 1], Op.mult)
    ts("c_bc", T.basec[:, :], T.oi[:, :], 512.0, Op.mult, 1024.0, Op.add)

    cn = MW * ((rank + 1) % n)
    vb = [T.pb0, T.pb1, T.pb5, T.pb7]
    need(pe, "c_y", "s_id")
    for j in range(n):
        q = (rank + j) % n
        if j == 1:
            need(pe, "c_sh", "l_h", "w_own", "s_sm", "sm_arr")
            pe.matmul(T.pb2[:, 0:4], T.sha[:, :], T.lf[:, :], True, False)
            inc(pe.matmul(T.pb2[:, 0:4], T.shb[0:8, :], T.sm[0:8, cn + 8:cn + 12], False, True), "p_halo")
        for b in range(8):
            inc(pe.matmul(vb[j][:, 64 * b:64 * b + 64], T.y[:, 128 * b:128 * b + 128], T.sm[:, MW * q + 16:MW * q + 80],
                          True, True), "p_v%d" % j)
        if j < n - 1:
            need(act, "p_v%d" % j)
            inc(act.activation(T.v[:, M * q:M * q + M], vb[j][:, :], Act.Copy), "v_in")
    need(v, "p_halo")
    inc(v.tensor_copy(T.li[:, 48:52], T.pb2[:, 0:4]), "l_hx")
    inc(v.tensor_copy(T.lx[:, 48:52], T.pb2[:, 0:4]), "l_hx")
    need(v, "sm_arr", "s_sm")
    inc(v.tensor_reduce(T.rootc[:, :], T.sm[:, 0:MW * n:MW], AxisListType.X, Op.add), "r_col")
    need(v, "l_hx", "c_u")
    inc(v.tensor_tensor(T.ls[:, 24:48], T.lm[:, 24:48], T.li[:, 25:49], Op.add), "l_e2")
    inc(v.tensor_copy(T.e[:, S:S + 64], T.u[:, 0:16].indirect(T.lx[:, 48:52])), "e_halo")
    need(v, "l_e2")
    inc(v.tensor_copy(T.letl[:, 24:48], T.ls[:, 24:48]), "l_l2")
    need(v, "r_col", "c_bc")
    ts("r_all", T.rall[:, 0:1], T.rootc[:, :], T.basec[:, :], Op.add)
    need(v, "p_v%d" % (n - 1))
    inc(v.tensor_copy(T.v[:, M * q:M * q + M], vb[n - 1][:, :]), "v_in2")

    win, win2 = T.w[:, 0:4 * M], T.v[:, 0:4 * M]
    lbank = {"a": T.pb2, "b": T.pb3}
    zb = {1: T.pb0, 2: T.pb1, 3: T.pb5, 4: T.pb7}
    z5 = {"a": T.pb4, "b": T.pb6}
    part = {"a": 0, "b": 1}

    def step(k, f):
        h = part[f]
        src = T.r[:, 0:4 * R].indirect(T.letl[:, 24 * h:24 * h + 24]) if k == 2 else \
            win.indirect(T["list%d" % k][:, 24 * h:24 * h + 24])
        inc(v.tensor_tensor(T["m%d" % k][:, H * h:H * h + H], src, T.e[:, 16 * k + H * h:16 * k + H * h + H], Op.mult),
            "v_m%d%s" % (k, f))

    def wrap(k, f):
        h = part[f]
        if k > 2:
            need(pe, "v_list%d%s" % (k, f))
        out = lbank[f][:, 0:24]
        pe.matmul(out, T.idb[:, :], T.base[:, 24 * h:24 * h + 24], True, False)
        need(pe, "v_m%d%s" % (k, f))
        for i in range(16):
            call = pe.matmul(out, T.sel[:, 128 * i:128 * i + 128], T["m%d" % k][:, H * h + i:H * h + H:16], False, i == 15)
        inc(call, "p_list%d%s" % (k + 1, f))

    def take(k, f):
        h = part[f]
        need(v, "p_list%d%s" % (k, f))
        inc(v.tensor_copy(T["list%d" % k][:, 24 * h:24 * h + 24], lbank[f][:, 0:24]), "v_list%d%s" % (k, f))
        need(v, "v_list%d%s" % (k, f))

    def add_far(k, z):
        pe.matmul(z, T.far[0:k, :], T.ones[0:k, 0:z.shape[1]], True, False)

    def sums(k, z, col, s, last):
        for b in range(4):
            i = 4 * b + s
            call = pe.matmul(z[0:32, col:col + 48], T.sel[:, 128 * i + s:128 * i + 128:4], T["a%d" % k][:, i:S:16],
                             False, last and b == 3)
        return call

    def ids(k, *waits):
        need(pe, *waits)
        for s in range(4):
            call = sums(k, zb[k], 48 * s, s, s == 3)
        inc(call, "p_z%d" % k)

    def keep(k):
        need(v, "p_z%d" % k, "d%d" % (k - 1))
        inc(v.tensor_tensor(T.best[0:32, :], zb[k][0:32, 0:192], T.best[0:32, :], Op.max), "d%d" % k)

    need(act, "v_in", "v_in2", "r_all")
    inc(act.activation(T.rid[:, :], win2.indirect(T.rall[:, 0:1]), Act.Copy), "a_rid")
    need(act, "a_rid")
    inc(act.activation(T.a1[:, :], T.rid[:, 0:16].indirect(T.lx[:, 0:48]), Act.Copy), "a_id1")
    need(v, "r_arr", "l_l", "e_main")
    step(2, "a")
    need(v, "l_l2", "e_halo")
    step(2, "b")
    need(v, "z_rl")
    for q in range(n):
        ts("r_l", T.rl[:, 5 * q:5 * q + 4], T.r[:, R * q + 64 + 4 * q:R * q + 68 + 4 * q], 256.0 + M * q, Op.add)
    need(act, "r_l")
    inc(act.activation(T.ridb[:, :], win2.indirect(T.rl[:, 0:20]), Act.Copy), "a_ridb")
    need(act, "a_ridb", "l_l", "l_l2")
    inc(act.activation(T.a2[:, :], T.ridb[:, 0:4 * R].indirect(T.letl[:, 0:48]), Act.Copy), "a_id2")
    need(pe, "b_base", "c_sel", "l_hx", "z_ones")
    for f in "ab":
        add_far(5, z5[f][0:32, 0:96])
    wrap(2, "a")
    wrap(2, "b")
    need(pe, "v_in", "v_in2")
    for k in (1, 2, 3, 4):
        add_far(k, zb[k][0:32, 0:192])
    ids(1, "a_id1")
    take(3, "a")
    take(3, "b")
    need(act, "v_list3a", "v_list3b")
    inc(act.activation(T.a3[:, :], win2.indirect(T.list3[:, 0:48]), Act.Copy), "a_id3")
    need(v, "w_arr")
    step(3, "a")
    step(3, "b")
    wrap(3, "a")
    wrap(3, "b")
    ids(2, "a_id2")
    for f in "ab":
        take(4, f)
        step(4, f)
        h = part[f]
        need(act, "v_list4" + f)
        inc(act.activation(T.a4[:, H * h:H * h + H], win2.indirect(T.list4[:, 24 * h:24 * h + 24]), Act.Copy), "a_id4" + f)
        wrap(4, f)
    ids(3, "a_id3")
    ids(4, "a_id4a", "a_id4b")
    need(act, "p_z1")
    inc(act.activation(T.best[0:32, :], zb[1][0:32, 0:192], Act.Relu), "d1")
    need(v, "v_in", "v_in2")
    take(5, "a")
    inc(v.tensor_copy(T.a5[:, 0:H], win2.indirect(T.list5[:, 0:24])), "v_id5a")
    take(5, "b")
    inc(v.tensor_copy(T.a5[:, H:H + 192], win2.indirect(T.list5[:, 24:36])), "v_id5b")
    need(act, "v_list5b")
    inc(act.activation(T.a5[:, H + 192:S], win2.indirect(T.list5[:, 36:48]), Act.Copy), "a_id5")
    for k in (2, 3, 4):
        keep(k)
    need(pe, "v_id5a", "v_id5b", "a_id5")
    for f in "ab":
        for j in range(2):
            call = sums(5, z5[f], 48 * j, 2 * part[f] + j, j == 1)
        inc(call, "p_z5" + f)

    half = {f: slice(96 * part[f], 96 * part[f] + 96) for f in "ab"}
    for f in "ab":
        need(v, "p_z5" + f, "d4")
        inc(v.tensor_tensor(T.pb2[0:32, half[f]], z5[f][0:32, 0:96], T.best[0:32, half[f]], Op.max), "d5" + f)
    for f in "ab":
        need(v, "d5" + f)
        ts("rr_ok" + f, T.rr[0:32, half[f]], T.pb2[0:32, half[f]], BIG, Op.add, -BIG, Op.add)
    for f in "ab":
        need(v, "rr_ok" + f)
        inc(v.tensor_tensor(T.yi[0:32, half[f]], T.pb2[0:32, half[f]], T.rr[0:32, half[f]], Op.subtract), "yi_ok" + f)
        need(act, "rr_ok" + f)
        inc(act.activation(T.yl[0:32, half[f]], T.rr[0:32, half[f]], Act.Copy, scale=1.0 / C), "yl_ok" + f)
    need(act, "yl_oka", "yl_okb")
    inc(act.dma_start(T.ylen[:, :], T.yl[0:32, :]), "st_len", 16)
    need(sp, "yi_oka", "yi_okb")
    inc(sp.dma_start(T.yid[:, :], T.yi[0:32, :]), "st_id", 16)
    need(act, "st_len")
    need(sp, "st_id")
    need(g, "sm_out", "w_out", "r_out")
